import numpy as np
import ml_dtypes


def mxq(x, axis, fmt="e4m3"):
    dtype, down = {"e4m3": (ml_dtypes.float8_e4m3fn, 7), "e5m2": (ml_dtypes.float8_e5m2, 14)}[fmt]
    v = np.moveaxis(np.asarray(x, np.float32).astype(ml_dtypes.bfloat16).astype(np.float64), axis, -1)
    blocks = v.reshape(v.shape[:-1] + (-1, 32))
    amax = np.abs(blocks).max(-1, keepdims=True)
    byte = np.maximum(np.where(amax > 0, np.frexp(amax)[1] - 1 + 127, 0) - down, 1)
    scale = np.exp2(byte - 127.0)
    codes = (blocks / scale).astype(np.float32).astype(dtype).astype(np.float64)
    return np.moveaxis((codes * scale).reshape(v.shape), -1, axis)


WIDE = False


def mx_kscale(k):
    if not WIDE:
        return np.ones(k)
    levels = np.array([10, -10, 5, -5, 0])
    if k % 512:
        return np.exp2(np.random.permutation(np.resize(levels, k // 32))).repeat(32)
    a = np.empty((k // 512, 16))
    for p in range(k // 512):
        a[p, :8] = np.random.permutation(np.resize(levels, 8))
        for g in range(8):
            far = levels[np.abs(levels - a[p, g]) >= 10]
            a[p, g + 8] = far[np.random.randint(len(far))]
    return np.exp2(a.ravel()).repeat(32)


def f64(x):
    return np.asarray(x).astype(np.float64)


def striped(idx):
    return np.tile(idx.reshape(-1, 16).T, (8, 1)).astype(np.uint16)


def unstriped(offs):
    return offs[:16].T.reshape(-1).astype(np.int64)


E2M1 = np.array([0.0, 0.5, 1.0, 1.5, 2.0, 3.0, 4.0, 6.0, -0.0, -0.5, -1.0, -1.5, -2.0, -3.0, -4.0, -6.0])


def pack_weight(w, fmt):
    k, n = w.shape
    w = f64(np.asarray(w, np.float32).astype(ml_dtypes.bfloat16)).reshape(k // 32, 32, n)
    amax = np.abs(w).max(1)
    if fmt == "e4m3":
        byte = np.frexp(amax)[1] - 1 + 127 - 7
    else:
        mant, ex = np.frexp(amax / 6.0)
        byte = np.where(mant > 0.5, ex, ex - 1) + 127
    byte = np.clip(np.where(amax > 0, byte, 1), 1, 254)
    scaled = (w * np.exp2(127.0 - byte)[:, None, :]).reshape(k, n).astype(np.float32)
    by_word = np.ascontiguousarray(scaled.reshape(k // 512, 128, 4, n).transpose(0, 1, 3, 2))
    if fmt == "e4m3":
        words = by_word.astype(ml_dtypes.float8_e4m3fn).view(np.uint8)
    else:
        c = by_word.astype(ml_dtypes.float4_e2m1fn).view(np.uint8) & 0xF
        words = (c[..., 0::2] | (c[..., 1::2] << 4)).reshape(k // 512, 128, 2 * n)
    return np.ascontiguousarray(words), np.ascontiguousarray(byte.astype(np.uint8).reshape(k // 512, 16, n))


def unpack_weight(words, scales, fmt):
    g, _, n = scales.shape
    words = np.ascontiguousarray(words).reshape(g, 128, n, -1)
    if fmt == "e4m3":
        vals = words.view(ml_dtypes.float8_e4m3fn).astype(np.float64)
    else:
        nib = np.empty((g, 128, n, 4), np.uint8)
        nib[..., 0::2] = words & 0xF
        nib[..., 1::2] = words >> 4
        vals = E2M1[nib]
    vals = vals * np.repeat(np.exp2(scales.astype(np.float64) - 127.0), 8, axis=1)[..., None]
    return vals.transpose(0, 1, 3, 2).reshape(g * 512, n)


K, T, E, C, N = 1024, 768, 12, 128, 256


def by_expert(wq, xq):
    return np.concatenate([wq[e].T @ xq[:, e * C:(e + 1) * C] for e in range(E)], axis=1)


def setup_inputs():
    n = np.random.standard_normal
    s = mx_kscale(K)
    first = np.random.permutation(np.repeat(np.arange(E), T // E))
    second = (first + 1 + np.random.permutation(np.repeat(np.arange(E - 1), -(-T // (E - 1)))[:T])) % E
    while np.bincount(second, minlength=E).max() != T // E:
        load = np.bincount(second, minlength=E); hi, lo = int(load.argmax()), int(load.argmin())
        t = np.flatnonzero((second == hi) & (first != lo))[0]; second[t] = lo
    slot_token = np.empty(E * C, np.int64); pos = np.empty((2, T), np.int64); fill = np.zeros(E, np.int64)
    place = np.stack([np.random.permutation(C) for _ in range(E)])
    for r, deal in enumerate((first, second)):
        for t in np.random.permutation(T):
            e = deal[t]; j = e * C + place[e, fill[e]]; fill[e] += 1; slot_token[j] = t; pos[r, t] = j
    g = np.random.uniform(0.2, 0.8, T)
    x = pack_weight(n((K, T)) * s[:, None], "e4m3")
    wq = [pack_weight(m, "e2m1") for m in n((E, K, N)) / np.sqrt(K) / s[None, :, None]]
    wk = [pack_weight(m, "e4m3") for m in n((E, K, N)) / np.sqrt(K) / s[None, :, None]]
    return {
        "x_words": x[0],
        "x_scales": x[1],
        "wq_words": np.stack([m[0] for m in wq]),
        "wq_scales": np.stack([m[1] for m in wq]),
        "wk_words": np.stack([m[0] for m in wk]),
        "wk_scales": np.stack([m[1] for m in wk]),
        "wv": (n((E, K, N)) / np.sqrt(K) / s[None, :, None]).astype(np.float32),
        "bias": (0.3 * n((3 * N, E))).astype(np.float32),
        "gate": np.stack([np.tile(g, (128, 1)), np.tile(1.0 - g, (128, 1))]).astype(np.float32),
        "offs": striped(slot_token),
        "pos1": striped(pos[0]),
        "pos2": striped(pos[1]),
    }


def reference(x_words, x_scales, wq_words, wq_scales, wk_words, wk_scales, wv, bias, gate, offs, pos1, pos2):
    wq = np.stack([unpack_weight(wq_words[e], wq_scales[e], "e2m1") for e in range(E)])
    wk = np.stack([unpack_weight(wk_words[e], wk_scales[e], "e4m3") for e in range(E)])
    wvq = mxq(f64(wv), 1, "e4m3")
    idx = unstriped(offs)
    xq = unpack_weight(x_words, x_scales, "e4m3")[:, idx]
    y = np.concatenate([by_expert(w, xq) for w in (wq, wk, wvq)])
    y = y + np.repeat(f64(bias), C, axis=1)
    out = sum(f64(gate[r, :1]) * y[:, unstriped(p)] for r, p in enumerate((pos1, pos2)))
    return out

@@ -1,0 +1,209 @@
+from contextlib import ExitStack
+
+import concourse.mybir as mybir
+
+K, T, E, C, N = 1024, 768, 12, 128, 256
+S = E * C
+FLOPS = 2 * K * 3 * N * S
+
+F32 = mybir.dt.float32
+BF16 = mybir.dt.bfloat16
+I32 = mybir.dt.int32
+U32 = mybir.dt.uint32
+U16 = mybir.dt.uint16
+U8 = mybir.dt.uint8
+FP8X4 = mybir.dt.float8_e4m3fn_x4
+FP4X4 = mybir.dt.float4_e2m1fn_x4
+MULT = mybir.AluOpType.mult
+ADD = mybir.AluOpType.add
+IDENTITY = mybir.ActivationFunctionType.Identity
+
+P = 128
+PASSES = 2
+GROUP = 4
+GROUPS = E // GROUP
+GSLOTS = GROUP * C
+SPLIT = 4
+
+
+def tile_moe_qkv_kernel(
+    tc, x_words, x_scales, wq_words, wq_scales, wk_words, wk_scales, wv, bias, gate, offs, pos1, pos2, out
+):
+    nc = tc.nc
+    with ExitStack() as ctx:
+        lists = ctx.enter_context(tc.tile_pool(name="lists", bufs=1))
+        keep = ctx.enter_context(tc.tile_pool(name="keep", bufs=1))
+        ring = ctx.enter_context(tc.tile_pool(name="ring", bufs=1))
+        psum = ctx.enter_context(tc.psum_pool(name="psum", bufs=8))
+
+        offs_sb = lists.tile([P, S // 16], U16, name="offs_sb")
+        pos_sb = [lists.tile([P, T // 16], U16, name="pos%d_sb" % r) for r in range(2)]
+
+        xw = [keep.tile([P, T], U32, name="xw%d" % s, align_bytes=64) for s in range(PASSES)]
+        xs = keep.tile([P, T], U8, name="xs", align_bytes=64)
+        xg = [keep.tile([P, S], U32, name="xg%d" % s, align_bytes=64) for s in range(PASSES)]
+        xsg = keep.tile([P, S], U8, name="xsg", align_bytes=64)
+        xs1 = keep.tile([P, S], U8, name="xs1", align_bytes=64)
+        wplanes = keep.tile([P, E * PASSES, N], U8, name="wplanes", align_bytes=64)
+        wq_sb = [keep.tile([P, GROUP * PASSES, 2 * N], U8, name="wq%d" % g, align_bytes=64) for g in range(GROUPS)]
+        wk_sb = [keep.tile([P, GROUP * PASSES, N], U32, name="wk%d" % g, align_bytes=64) for g in range(GROUPS)]
+        bias_sb = keep.tile([P, 6, E], F32, name="bias_sb")
+        gate_sb = [keep.tile([P, T], F32, name="gate%d" % r) for r in range(2)]
+        y = {}
+
+        nc.vector.memset(xs[:].bitcast(I32), 0)
+        nc.vector.memset(wplanes[:].rearrange("p a n -> p (a n)").bitcast(I32), 0)
+        nc.vector.memset(xs1[:].bitcast(I32), 0)
+
+        nc.sync.dma_start(offs_sb[:], offs)
+        for s in range(PASSES):
+            nc.sync.dma_start(xw[s][:].bitcast(I32), x_words[s].rearrange("p t d -> p (t d)").bitcast(I32))
+        for q in range(4):
+            nc.sync.dma_start(xs[32 * q : 32 * q + 8, :].bitcast(I32), x_scales[:, 4 * q : 4 * q + 4, :].bitcast(I32))
+        for first, scales in ((0, wq_scales), (4, wk_scales)):
+            by_row = scales.rearrange("e s (q r) n -> r q (e s) n", r=4)
+            for r in range(4):
+                nc.sync.dma_start(wplanes[first + r : P : 32, :, :].bitcast(I32), by_row[r].bitcast(I32))
+
+        def gather_words(g):
+            cols = slice(g * GSLOTS, (g + 1) * GSLOTS)
+            for s in range(PASSES):
+                nc.vector.tensor_copy(xg[s][:, cols], xw[s][:].indirect(offs_sb[:, g * 32 : (g + 1) * 32]))
+
+        def gather_scales(g):
+            cols = slice(g * GSLOTS, (g + 1) * GSLOTS)
+            nc.vector.tensor_copy(xsg[:, cols], xs[:].indirect(offs_sb[:, g * 32 : (g + 1) * 32]))
+
+        def load_wq(g):
+            src = wq_words[g * GROUP : (g + 1) * GROUP].rearrange("e s p b -> p (e s) b")
+            nc.sync.dma_start(wq_sb[g][:].bitcast(I32), src.bitcast(I32))
+
+        def load_wk(g):
+            src = wk_words[g * GROUP : (g + 1) * GROUP].rearrange("e s p n d -> p (e s) (n d)")
+            nc.sync.dma_start(wk_sb[g][:].bitcast(I32), src.bitcast(I32))
+
+        def y_tile(m):
+            if m not in y:
+                y[m] = ring.tile([P, S], F32, name="y", bufs=6)
+            return y[m]
+
+        def evacuate(m, e, acc):
+            nc.scalar.activation(y_tile(m)[:, e * C : (e + 1) * C], acc, IDENTITY, bias=bias_sb[:, m, e : e + 1])
+
+        def project_packed(first_m, g):
+            for h in range(2):
+                acc = psum.tile([P, GROUP, C], F32, name="acc")
+                for i in range(GROUP):
+                    e = g * GROUP + i
+                    slots = slice(e * C, (e + 1) * C)
+                    for s in range(PASSES):
+                        cols = slice(h * P, (h + 1) * P)
+                        if first_m == 0:
+                            lhsT = wq_sb[g][:, i * PASSES + s, 2 * h * P : 2 * (h + 1) * P].bitcast(FP4X4)
+                            lhsT_scale = wplanes[:, e * PASSES + s, cols]
+                            rhs_scale = (xsg, xs1)[s][:, slots]
+                        else:
+                            lhsT = wk_sb[g][:, i * PASSES + s, cols].bitcast(FP8X4)
+                            lhsT_scale = wplanes[4:P, e * PASSES + s, cols]
+                            rhs_scale = xsg[4 * s : P, slots]
+                        nc.tensor.matmul_mx(
+                            acc[:, i, :], lhsT=lhsT, lhsT_scale=lhsT_scale, rhs=xg[s][:, slots].bitcast(FP8X4),
+                            rhs_scale=rhs_scale, start=(s == 0), stop=(s == PASSES - 1),
+                        )
+                for i in range(GROUP):
+                    evacuate(first_m + h, g * GROUP + i, acc[:, i, :])
+
+        raw = {}
+
+        def load_wv(e, halves):
+            width = P * len(halves)
+            t = ring.tile([P, PASSES, 4, width], F32, name="wv_raw", bufs=9)
+            src = wv[e].rearrange("(s p j) n -> p s j n", p=P, j=4)[:, :, :, halves[0] * P : halves[0] * P + width]
+            if width == N:
+                nc.sync.dma_start(t[:].rearrange("p s j n -> p s (j n)"), src.rearrange("p s j n -> p s (j n)"))
+            else:
+                for s in range(PASSES):
+                    nc.sync.dma_start(t[:, s, :, :], src[:, s, :, :])
+            raw[e, halves] = t
+
+        def project_v(e, halves, vector_passes):
+            width = P * len(halves)
+            t = raw[e, halves]
+            rounded = ring.tile([P, PASSES, width, 4], BF16, name="rounded", bufs=5, align_bytes=64)
+            for s in range(PASSES):
+                dst = rounded[:, s, :, :].rearrange("p (c i) j -> p c j i", i=4)
+                src = t[:, s, :, :].rearrange("p j (c i) -> p c j i", i=4)
+                if s in vector_passes:
+                    nc.vector.tensor_copy(dst, src)
+                else:
+                    nc.scalar.copy(dst, src)
+            codes = ring.tile([P, PASSES, width], U32, name="codes", bufs=3, align_bytes=64)
+            plane = ring.tile([P, PASSES, width], U8, name="plane", bufs=3, align_bytes=64)
+            nc.vector.quantize_mx(
+                codes[:].rearrange("p s n -> p (s n)").bitcast(FP8X4),
+                plane[:].rearrange("p s n -> p (s n)"),
+                rounded[:].rearrange("p s n j -> p (s n j)"),
+            )
+            slots = slice(e * C, (e + 1) * C)
+            acc = psum.tile([P, GROUP, C], F32, name="acc")
+            for i, h in enumerate(halves):
+                cols = slice(i * P, (i + 1) * P)
+                for s in range(PASSES):
+                    nc.tensor.matmul_mx(
+                        acc[:, i, :], lhsT=codes[:, s, cols].bitcast(FP8X4), lhsT_scale=plane[:, s, cols],
+                        rhs=xg[s][:, slots].bitcast(FP8X4), rhs_scale=xsg[4 * s : P, slots],
+                        start=(s == 0), stop=(s == PASSES - 1),
+                    )
+            for i, h in enumerate(halves):
+                evacuate(4 + h, e, acc[:, i, :])
+
+        def combine(m, pieces):
+            width = T // pieces
+            first = ring.tile([P, T], F32, name="first", bufs=6)
+            second = ring.tile([P, T], F32, name="second", bufs=2)
+            for c in range(pieces):
+                cols = slice(c * width, (c + 1) * width)
+                lcols = slice(c * width // 16, (c + 1) * width // 16)
+                for r, dst in enumerate((first, second)):
+                    nc.vector.tensor_tensor(dst[:, cols], y[m][:].indirect(pos_sb[r][:, lcols]), gate_sb[r][:, cols], MULT)
+            for c in range(pieces):
+                cols = slice(c * width, (c + 1) * width)
+                nc.vector.tensor_tensor(first[:, cols], first[:, cols], second[:, cols], ADD)
+                nc.sync.dma_start(out[m * P : (m + 1) * P, cols], first[:, cols])
+
+        both = (0, 1)
+        for r, pos in enumerate((pos1, pos2)):
+            nc.sync.dma_start(pos_sb[r][:], pos)
+        nc.sync.dma_start(bias_sb[:], bias.rearrange("(m p) e -> p m e", p=P))
+        load_wv(0, both)
+        for g in range(GROUPS):
+            load_wq(g)
+        for r in range(2):
+            nc.sync.dma_start(gate_sb[r][:], gate[r])
+        for e in (1, 2, 3):
+            load_wv(e, both)
+        for g in range(GROUPS):
+            load_wk(g)
+            load_wv(4 + g, both)
+        load_wv(7, both)
+
+        gather_words(0)
+        for g in range(GROUPS):
+            gather_scales(g)
+        for r in range(4):
+            nc.scalar.dma_start(xs1[r:P:32, :].bitcast(I32), xsg[4 + r : P : 32, :].bitcast(I32))
+        for g in range(1, GROUPS):
+            gather_words(g)
+        for e in range(E - SPLIT):
+            project_v(e, both, (1,) if e % 2 == 1 else ())
+            if e == 0:
+                for g in range(GROUPS):
+                    project_packed(0, g)
+            if e in (4, 5, 6):
+                project_packed(2, e - 4)
+        for h in range(2):
+            for e in range(E - SPLIT, E):
+                load_wv(e, (h,))
+                project_v(e, (h,), (1,) if (h == 1 and e == E - 1) else ())
+        for m in range(6):
+            combine(m, 2)

@@ -40,30 +40,21 @@ def tile_moe_qkv_kernel(
         pos_sb = [lists.tile([P, T // 16], U16, name="pos%d_sb" % r) for r in range(2)]
 
         xw = [keep.tile([P, T], U32, name="xw%d" % s, align_bytes=64) for s in range(PASSES)]
-        xs = keep.tile([P, T], U8, name="xs", align_bytes=64)
+        xs = keep.tile([P, PASSES, T], U8, name="xs", align_bytes=64)
         xg = [keep.tile([P, S], U32, name="xg%d" % s, align_bytes=64) for s in range(PASSES)]
-        xsg = keep.tile([P, S], U8, name="xsg", align_bytes=64)
-        xs1 = keep.tile([P, S], U8, name="xs1", align_bytes=64)
+        xsg = [keep.tile([P, S], U8, name="xsg%d" % s, align_bytes=64) for s in range(PASSES)]
         wplanes = keep.tile([P, E * PASSES, N], U8, name="wplanes", align_bytes=64)
-        wq_sb = [keep.tile([P, GROUP * PASSES, 2 * N], U8, name="wq%d" % g, align_bytes=64) for g in range(GROUPS)]
+        wq_sb = [ring.tile([P, GROUP * PASSES, 2 * N], U8, name="wq", bufs=GROUPS, align_bytes=64) for g in range(GROUPS)]
         wk_sb = [keep.tile([P, GROUP * PASSES, N], U32, name="wk%d" % g, align_bytes=64) for g in range(GROUPS)]
         bias_sb = keep.tile([P, 6, E], F32, name="bias_sb")
         gate_sb = [keep.tile([P, T], F32, name="gate%d" % r) for r in range(2)]
         y = {}
 
-        nc.vector.memset(xs[:].bitcast(I32), 0)
-        nc.vector.memset(wplanes[:].rearrange("p a n -> p (a n)").bitcast(I32), 0)
-        nc.vector.memset(xs1[:].bitcast(I32), 0)
-
-        nc.sync.dma_start(offs_sb[:], offs)
-        for s in range(PASSES):
-            nc.sync.dma_start(xw[s][:].bitcast(I32), x_words[s].rearrange("p t d -> p (t d)").bitcast(I32))
-        for q in range(4):
-            nc.sync.dma_start(xs[32 * q : 32 * q + 8, :].bitcast(I32), x_scales[:, 4 * q : 4 * q + 4, :].bitcast(I32))
-        for first, scales in ((0, wq_scales), (4, wk_scales)):
-            by_row = scales.rearrange("e s (q r) n -> r q (e s) n", r=4)
-            for r in range(4):
-                nc.sync.dma_start(wplanes[first + r : P : 32, :, :].bitcast(I32), by_row[r].bitcast(I32))
+        plane_words = wplanes[:].rearrange("p a n -> p (a n)").bitcast(I32)
+        half_words = E * PASSES * N // 8
+        nc.gpsimd.memset(xs[:].rearrange("p s t -> p (s t)").bitcast(I32), 0)
+        nc.vector.memset(plane_words[:, :half_words], 0)
+        nc.gpsimd.memset(plane_words[:, half_words:], 0)
 
         def gather_words(g):
             cols = slice(g * GSLOTS, (g + 1) * GSLOTS)
@@ -72,7 +63,8 @@ def tile_moe_qkv_kernel(
 
         def gather_scales(g):
             cols = slice(g * GSLOTS, (g + 1) * GSLOTS)
-            nc.vector.tensor_copy(xsg[:, cols], xs[:].indirect(offs_sb[:, g * 32 : (g + 1) * 32]))
+            for s in range(PASSES):
+                nc.vector.tensor_copy(xsg[s][:, cols], xs[:, s, :].indirect(offs_sb[:, g * 32 : (g + 1) * 32]))
 
         def load_wq(g):
             src = wq_words[g * GROUP : (g + 1) * GROUP].rearrange("e s p b -> p (e s) b")
@@ -84,14 +76,17 @@ def tile_moe_qkv_kernel(
 
         def y_tile(m):
             if m not in y:
-                y[m] = ring.tile([P, S], F32, name="y", bufs=6)
+                if m in (2, 3):
+                    y[m] = ring.tile([P, S], F32, name="wv_raw", bufs=E - SPLIT, align_bytes=64)
+                else:
+                    y[m] = keep.tile([P, S], F32, name="y%d" % m)
             return y[m]
 
         def evacuate(m, e, acc):
             nc.scalar.activation(y_tile(m)[:, e * C : (e + 1) * C], acc, IDENTITY, bias=bias_sb[:, m, e : e + 1])
 
-        def project_packed(first_m, g):
-            for h in range(2):
+        def project_packed(first_m, g, halves):
+            for h in halves:
                 acc = psum.tile([P, GROUP, C], F32, name="acc")
                 for i in range(GROUP):
                     e = g * GROUP + i
@@ -101,14 +96,12 @@ def tile_moe_qkv_kernel(
                         if first_m == 0:
                             lhsT = wq_sb[g][:, i * PASSES + s, 2 * h * P : 2 * (h + 1) * P].bitcast(FP4X4)
                             lhsT_scale = wplanes[:, e * PASSES + s, cols]
-                            rhs_scale = (xsg, xs1)[s][:, slots]
                         else:
                             lhsT = wk_sb[g][:, i * PASSES + s, cols].bitcast(FP8X4)
                             lhsT_scale = wplanes[4:P, e * PASSES + s, cols]
-                            rhs_scale = xsg[4 * s : P, slots]
                         nc.tensor.matmul_mx(
                             acc[:, i, :], lhsT=lhsT, lhsT_scale=lhsT_scale, rhs=xg[s][:, slots].bitcast(FP8X4),
-                            rhs_scale=rhs_scale, start=(s == 0), stop=(s == PASSES - 1),
+                            rhs_scale=xsg[s][:, slots], start=(s == 0), stop=(s == PASSES - 1),
                         )
                 for i in range(GROUP):
                     evacuate(first_m + h, g * GROUP + i, acc[:, i, :])
@@ -117,7 +110,10 @@ def tile_moe_qkv_kernel(
 
         def load_wv(e, halves):
             width = P * len(halves)
-            t = ring.tile([P, PASSES, 4, width], F32, name="wv_raw", bufs=9)
+            if width == N:
+                t = ring.tile([P, PASSES, 4, width], F32, name="wv_raw", bufs=E - SPLIT, align_bytes=64)
+            else:
+                t = ring.tile([P, PASSES, 4, width], F32, name="wv_half", bufs=2 * SPLIT, align_bytes=64)
             src = wv[e].rearrange("(s p j) n -> p s j n", p=P, j=4)[:, :, :, halves[0] * P : halves[0] * P + width]
             if width == N:
                 nc.sync.dma_start(t[:].rearrange("p s j n -> p s (j n)"), src.rearrange("p s j n -> p s (j n)"))
@@ -151,7 +147,7 @@ def tile_moe_qkv_kernel(
                 for s in range(PASSES):
                     nc.tensor.matmul_mx(
                         acc[:, i, :], lhsT=codes[:, s, cols].bitcast(FP8X4), lhsT_scale=plane[:, s, cols],
-                        rhs=xg[s][:, slots].bitcast(FP8X4), rhs_scale=xsg[4 * s : P, slots],
+                        rhs=xg[s][:, slots].bitcast(FP8X4), rhs_scale=xsg[s][:, slots],
                         start=(s == 0), stop=(s == PASSES - 1),
                     )
             for i, h in enumerate(halves):
@@ -159,7 +155,10 @@ def tile_moe_qkv_kernel(
 
         def combine(m, pieces):
             width = T // pieces
-            first = ring.tile([P, T], F32, name="first", bufs=6)
+            if m < GROUPS:
+                first = ring.tile([P, T], F32, name="wq", bufs=GROUPS, align_bytes=64)
+            else:
+                first = ring.tile([P, T], F32, name="wv_raw", bufs=E - SPLIT, align_bytes=64)
             second = ring.tile([P, T], F32, name="second", bufs=2)
             for c in range(pieces):
                 cols = slice(c * width, (c + 1) * width)
@@ -172,38 +171,49 @@ def tile_moe_qkv_kernel(
                 nc.sync.dma_start(out[m * P : (m + 1) * P, cols], first[:, cols])
 
         both = (0, 1)
+        nc.sync.dma_start(offs_sb[:], offs)
+        for s in range(PASSES):
+            nc.sync.dma_start(xw[s][:].bitcast(I32), x_words[s].rearrange("p t d -> p (t d)").bitcast(I32))
+        load_wv(0, both)
+        load_wv(1, both)
         for r, pos in enumerate((pos1, pos2)):
             nc.sync.dma_start(pos_sb[r][:], pos)
         nc.sync.dma_start(bias_sb[:], bias.rearrange("(m p) e -> p m e", p=P))
-        load_wv(0, both)
+        x_by_row = x_scales.rearrange("s (q r) t -> r q s t", r=4)
+        for r in range(4):
+            nc.sync.dma_start(xs[r:P:32, :, :].bitcast(I32), x_by_row[r].bitcast(I32))
+        for r in range(4):
+            for first, scales in ((0, wq_scales), (4, wk_scales)):
+                by_row = scales.rearrange("e s (q r) n -> r q (e s) n", r=4)
+                nc.sync.dma_start(wplanes[first + r : P : 32, :, :].bitcast(I32), by_row[r].bitcast(I32))
         for g in range(GROUPS):
             load_wq(g)
         for r in range(2):
             nc.sync.dma_start(gate_sb[r][:], gate[r])
-        for e in (1, 2, 3):
-            load_wv(e, both)
+        load_wv(2, both)
+        load_wv(3, both)
         for g in range(GROUPS):
             load_wk(g)
-            load_wv(4 + g, both)
-        load_wv(7, both)
-
-        gather_words(0)
-        for g in range(GROUPS):
-            gather_scales(g)
-        for r in range(4):
-            nc.scalar.dma_start(xs1[r:P:32, :].bitcast(I32), xsg[4 + r : P : 32, :].bitcast(I32))
-        for g in range(1, GROUPS):
-            gather_words(g)
-        for e in range(E - SPLIT):
-            project_v(e, both, (1,) if e % 2 == 1 else ())
-            if e == 0:
-                for g in range(GROUPS):
-                    project_packed(0, g)
-            if e in (4, 5, 6):
-                project_packed(2, e - 4)
+        for e in range(4, E - SPLIT):
+            load_wv(e, both)
         for h in range(2):
             for e in range(E - SPLIT, E):
                 load_wv(e, (h,))
-                project_v(e, (h,), (1,) if (h == 1 and e == E - 1) else ())
+
+        for g in range(GROUPS):
+            gather_words(g)
+        for g in range(GROUPS):
+            gather_scales(g)
+        for h in range(2):
+            for g in range(GROUPS):
+                project_packed(0, g, (h,))
+        for e in range(E - SPLIT):
+            project_v(e, both, ())
+            if e == 3:
+                for g in range(GROUPS):
+                    project_packed(2, g, both)
+        for h in range(2):
+            for e in range(E - SPLIT, E):
+                project_v(e, (h,), (1,) if (h == 0 or e == E - 1) else ())
         for m in range(6):
-            combine(m, 2)
+            combine(m, 1 if m < 4 else 2)

@@ -34,7 +34,7 @@ def tile_moe_qkv_kernel(
         lists = ctx.enter_context(tc.tile_pool(name="lists", bufs=1))
         keep = ctx.enter_context(tc.tile_pool(name="keep", bufs=1))
         ring = ctx.enter_context(tc.tile_pool(name="ring", bufs=1))
-        psum = ctx.enter_context(tc.psum_pool(name="psum", bufs=8))
+        psum = ctx.enter_context(tc.psum_pool(name="psum", bufs=1))
 
         offs_sb = lists.tile([P, S // 16], U16, name="offs_sb")
         pos_sb = [lists.tile([P, T // 16], U16, name="pos%d_sb" % r) for r in range(2)]
@@ -43,18 +43,29 @@ def tile_moe_qkv_kernel(
         xs = keep.tile([P, PASSES, T], U8, name="xs", align_bytes=64)
         xg = [keep.tile([P, S], U32, name="xg%d" % s, align_bytes=64) for s in range(PASSES)]
         xsg = [keep.tile([P, S], U8, name="xsg%d" % s, align_bytes=64) for s in range(PASSES)]
-        wplanes = keep.tile([P, E * PASSES, N], U8, name="wplanes", align_bytes=64)
-        wq_sb = [ring.tile([P, GROUP * PASSES, 2 * N], U8, name="wq", bufs=GROUPS, align_bytes=64) for g in range(GROUPS)]
-        wk_sb = [keep.tile([P, GROUP * PASSES, N], U32, name="wk%d" % g, align_bytes=64) for g in range(GROUPS)]
+        qplanes = keep.tile([P, E * PASSES, N], U8, name="qplanes", align_bytes=64)
+        kplanes = keep.tile([P, E * PASSES, N], U8, name="kplanes", align_bytes=64)
+        wq_sb = [keep.tile([P, GROUP * PASSES, 2 * N], U8, name="wq%d" % g, align_bytes=64) for g in range(GROUPS)]
+        wk_sb = [
+            [keep.tile([P, GROUP * PASSES, P], U32, name="wk%d_%d" % (h, g), align_bytes=64) for g in range(GROUPS)]
+            for h in range(2)
+        ]
         bias_sb = keep.tile([P, 6, E], F32, name="bias_sb")
         gate_sb = [keep.tile([P, T], F32, name="gate%d" % r) for r in range(2)]
         y = {}
+        banks = [psum.tile([P, GROUP, C], F32, name="bank%d" % b) for b in range(8)]
 
-        plane_words = wplanes[:].rearrange("p a n -> p (a n)").bitcast(I32)
+        q_words = qplanes[:].rearrange("p a n -> p (a n)").bitcast(I32)
         half_words = E * PASSES * N // 8
         nc.gpsimd.memset(xs[:].rearrange("p s t -> p (s t)").bitcast(I32), 0)
-        nc.vector.memset(plane_words[:, :half_words], 0)
-        nc.gpsimd.memset(plane_words[:, half_words:], 0)
+        nc.vector.memset(q_words[:, :half_words], 0)
+        nc.gpsimd.memset(q_words[:, half_words:], 0)
+        nc.gpsimd.memset(kplanes[:].rearrange("p a n -> p (a n)").bitcast(I32), 0)
+
+        def load_planes(planes, first, scales):
+            by_row = scales.rearrange("e s (q r) n -> r q (e s) n", r=4)
+            for r in range(4):
+                nc.sync.dma_start(planes[first + r : P : 32, :, :].bitcast(I32), by_row[r].bitcast(I32))
 
         def gather_words(g):
             cols = slice(g * GSLOTS, (g + 1) * GSLOTS)
@@ -70,14 +81,14 @@ def tile_moe_qkv_kernel(
             src = wq_words[g * GROUP : (g + 1) * GROUP].rearrange("e s p b -> p (e s) b")
             nc.sync.dma_start(wq_sb[g][:].bitcast(I32), src.bitcast(I32))
 
-        def load_wk(g):
-            src = wk_words[g * GROUP : (g + 1) * GROUP].rearrange("e s p n d -> p (e s) (n d)")
-            nc.sync.dma_start(wk_sb[g][:].bitcast(I32), src.bitcast(I32))
+        def load_wk(h, g):
+            src = wk_words[g * GROUP : (g + 1) * GROUP, :, :, h * P : (h + 1) * P, :].rearrange("e s p n d -> p (e s) (n d)")
+            nc.sync.dma_start(wk_sb[h][g][:].bitcast(I32), src.bitcast(I32))
 
         def y_tile(m):
             if m not in y:
                 if m in (2, 3):
-                    y[m] = ring.tile([P, S], F32, name="wv_raw", bufs=E - SPLIT, align_bytes=64)
+                    y[m] = keep.tile([P, S], F32, name="wv%d_01" % (m - 2), align_bytes=64)
                 else:
                     y[m] = keep.tile([P, S], F32, name="y%d" % m)
             return y[m]
@@ -85,9 +96,9 @@ def tile_moe_qkv_kernel(
         def evacuate(m, e, acc):
             nc.scalar.activation(y_tile(m)[:, e * C : (e + 1) * C], acc, IDENTITY, bias=bias_sb[:, m, e : e + 1])
 
-        def project_packed(first_m, g, halves):
+        def project_packed(first_m, g, halves, bank):
             for h in halves:
-                acc = psum.tile([P, GROUP, C], F32, name="acc")
+                acc = banks[bank]
                 for i in range(GROUP):
                     e = g * GROUP + i
                     slots = slice(e * C, (e + 1) * C)
@@ -95,10 +106,10 @@ def tile_moe_qkv_kernel(
                         cols = slice(h * P, (h + 1) * P)
                         if first_m == 0:
                             lhsT = wq_sb[g][:, i * PASSES + s, 2 * h * P : 2 * (h + 1) * P].bitcast(FP4X4)
-                            lhsT_scale = wplanes[:, e * PASSES + s, cols]
+                            lhsT_scale = qplanes[:, e * PASSES + s, cols]
                         else:
-                            lhsT = wk_sb[g][:, i * PASSES + s, cols].bitcast(FP8X4)
-                            lhsT_scale = wplanes[4:P, e * PASSES + s, cols]
+                            lhsT = wk_sb[h][g][:, i * PASSES + s, :].bitcast(FP8X4)
+                            lhsT_scale = kplanes[4:P, e * PASSES + s, cols]
                         nc.tensor.matmul_mx(
                             acc[:, i, :], lhsT=lhsT, lhsT_scale=lhsT_scale, rhs=xg[s][:, slots].bitcast(FP8X4),
                             rhs_scale=xsg[s][:, slots], start=(s == 0), stop=(s == PASSES - 1),
@@ -110,10 +121,7 @@ def tile_moe_qkv_kernel(
 
         def load_wv(e, halves):
             width = P * len(halves)
-            if width == N:
-                t = ring.tile([P, PASSES, 4, width], F32, name="wv_raw", bufs=E - SPLIT, align_bytes=64)
-            else:
-                t = ring.tile([P, PASSES, 4, width], F32, name="wv_half", bufs=2 * SPLIT, align_bytes=64)
+            t = keep.tile([P, PASSES, 4, width], F32, name="wv%d_%s" % (e, "".join(map(str, halves))), align_bytes=64)
             src = wv[e].rearrange("(s p j) n -> p s j n", p=P, j=4)[:, :, :, halves[0] * P : halves[0] * P + width]
             if width == N:
                 nc.sync.dma_start(t[:].rearrange("p s j n -> p s (j n)"), src.rearrange("p s j n -> p s (j n)"))
@@ -122,7 +130,7 @@ def tile_moe_qkv_kernel(
                     nc.sync.dma_start(t[:, s, :, :], src[:, s, :, :])
             raw[e, halves] = t
 
-        def project_v(e, halves, vector_passes):
+        def project_v(e, halves, vector_passes, bank):
             width = P * len(halves)
             t = raw[e, halves]
             rounded = ring.tile([P, PASSES, width, 4], BF16, name="rounded", bufs=5, align_bytes=64)
@@ -133,15 +141,15 @@ def tile_moe_qkv_kernel(
                     nc.vector.tensor_copy(dst, src)
                 else:
                     nc.scalar.copy(dst, src)
-            codes = ring.tile([P, PASSES, width], U32, name="codes", bufs=3, align_bytes=64)
-            plane = ring.tile([P, PASSES, width], U8, name="plane", bufs=3, align_bytes=64)
+            codes = ring.tile([P, PASSES, width], U32, name="codes", bufs=5, align_bytes=64)
+            plane = ring.tile([P, PASSES, width], U8, name="plane", bufs=5, align_bytes=64)
             nc.vector.quantize_mx(
                 codes[:].rearrange("p s n -> p (s n)").bitcast(FP8X4),
                 plane[:].rearrange("p s n -> p (s n)"),
                 rounded[:].rearrange("p s n j -> p (s n j)"),
             )
             slots = slice(e * C, (e + 1) * C)
-            acc = psum.tile([P, GROUP, C], F32, name="acc")
+            acc = banks[bank]
             for i, h in enumerate(halves):
                 cols = slice(i * P, (i + 1) * P)
                 for s in range(PASSES):
@@ -153,52 +161,55 @@ def tile_moe_qkv_kernel(
             for i, h in enumerate(halves):
                 evacuate(4 + h, e, acc[:, i, :])
 
-        def combine(m, pieces):
-            width = T // pieces
-            if m < GROUPS:
-                first = ring.tile([P, T], F32, name="wq", bufs=GROUPS, align_bytes=64)
+        def combine(m, first_token, width, slots):
+            cols = slice(first_token, first_token + width)
+            lcols = slice(first_token // 16, (first_token + width) // 16)
+            if len(slots) == 1:
+                pair = keep.tile([P, 2, width], F32, name=slots[0], align_bytes=64)
+                terms = [pair[:, r, :] for r in range(2)]
             else:
-                first = ring.tile([P, T], F32, name="wv_raw", bufs=E - SPLIT, align_bytes=64)
-            second = ring.tile([P, T], F32, name="second", bufs=2)
-            for c in range(pieces):
-                cols = slice(c * width, (c + 1) * width)
-                lcols = slice(c * width // 16, (c + 1) * width // 16)
-                for r, dst in enumerate((first, second)):
-                    nc.vector.tensor_tensor(dst[:, cols], y[m][:].indirect(pos_sb[r][:, lcols]), gate_sb[r][:, cols], MULT)
-            for c in range(pieces):
-                cols = slice(c * width, (c + 1) * width)
-                nc.vector.tensor_tensor(first[:, cols], first[:, cols], second[:, cols], ADD)
-                nc.sync.dma_start(out[m * P : (m + 1) * P, cols], first[:, cols])
+                terms = [keep.tile([P, width], F32, name=slot, align_bytes=64)[:] for slot in slots]
+            for r in range(2):
+                nc.vector.tensor_tensor(terms[r], y[m][:].indirect(pos_sb[r][:, lcols]), gate_sb[r][:, cols], MULT)
+            nc.vector.tensor_tensor(terms[0], terms[0], terms[1], ADD)
+            nc.sync.dma_start(out[m * P : (m + 1) * P, cols], terms[0])
 
         both = (0, 1)
         nc.sync.dma_start(offs_sb[:], offs)
         for s in range(PASSES):
             nc.sync.dma_start(xw[s][:].bitcast(I32), x_words[s].rearrange("p t d -> p (t d)").bitcast(I32))
         load_wv(0, both)
-        load_wv(1, both)
-        for r, pos in enumerate((pos1, pos2)):
-            nc.sync.dma_start(pos_sb[r][:], pos)
-        nc.sync.dma_start(bias_sb[:], bias.rearrange("(m p) e -> p m e", p=P))
         x_by_row = x_scales.rearrange("s (q r) t -> r q s t", r=4)
         for r in range(4):
             nc.sync.dma_start(xs[r:P:32, :, :].bitcast(I32), x_by_row[r].bitcast(I32))
-        for r in range(4):
-            for first, scales in ((0, wq_scales), (4, wk_scales)):
-                by_row = scales.rearrange("e s (q r) n -> r q (e s) n", r=4)
-                nc.sync.dma_start(wplanes[first + r : P : 32, :, :].bitcast(I32), by_row[r].bitcast(I32))
-        for g in range(GROUPS):
-            load_wq(g)
-        for r in range(2):
-            nc.sync.dma_start(gate_sb[r][:], gate[r])
+        load_wv(1, both)
         load_wv(2, both)
         load_wv(3, both)
+        load_planes(qplanes, 0, wq_scales)
+        load_wq(0)
+        nc.sync.dma_start(bias_sb[:], bias.rearrange("(m p) e -> p m e", p=P))
+        load_wq(1)
+        load_wq(2)
+        for r, pos in enumerate((pos1, pos2)):
+            nc.sync.dma_start(pos_sb[r][:], pos)
+            nc.sync.dma_start(gate_sb[r][:], gate[r])
+        load_wv(4, both)
+        load_wv(5, both)
+        load_wv(6, both)
+        load_wv(7, both)
+        load_wv(8, (0,))
+        load_wv(9, (0,))
+        load_wv(10, (0,))
+        load_wv(11, (0,))
+        load_wv(8, (1,))
+        load_wv(9, (1,))
+        load_wv(10, (1,))
+        load_wv(11, (1,))
+        load_planes(kplanes, 4, wk_scales)
         for g in range(GROUPS):
-            load_wk(g)
-        for e in range(4, E - SPLIT):
-            load_wv(e, both)
-        for h in range(2):
-            for e in range(E - SPLIT, E):
-                load_wv(e, (h,))
+            load_wk(0, g)
+        for g in range(GROUPS):
+            load_wk(1, g)
 
         for g in range(GROUPS):
             gather_words(g)
@@ -206,14 +217,35 @@ def tile_moe_qkv_kernel(
             gather_scales(g)
         for h in range(2):
             for g in range(GROUPS):
-                project_packed(0, g, (h,))
-        for e in range(E - SPLIT):
-            project_v(e, both, ())
-            if e == 3:
-                for g in range(GROUPS):
-                    project_packed(2, g, both)
-        for h in range(2):
-            for e in range(E - SPLIT, E):
-                project_v(e, (h,), (1,) if (h == 0 or e == E - 1) else ())
-        for m in range(6):
-            combine(m, 1 if m < 4 else 2)
+                project_packed(0, g, (h,), GROUPS * h + g)
+        project_v(0, both, (), 5)
+        project_v(1, both, (), 5)
+        project_v(2, both, (), 5)
+        project_v(3, both, (), 5)
+        combine(0, 0, 384, ("wq0",))
+        combine(0, 384, 384, ("wq1",))
+        project_v(4, both, (), 6)
+        combine(1, 0, 384, ("wv4_01",))
+        project_v(5, both, (), 7)
+        combine(1, 384, 384, ("wv5_01",))
+        project_v(6, both, (1,), 6)
+        project_v(7, both, (1,), 7)
+        project_v(8, (0,), (1,), 6)
+        project_v(9, (0,), (1,), 7)
+        project_v(10, (0,), (1,), 6)
+        project_v(11, (0,), (1,), 7)
+        combine(4, 0, 256, ("wq2",))
+        project_v(8, (1,), (), 6)
+        project_v(9, (1,), (), 7)
+        combine(4, 256, 256, ("wv9_1",))
+        project_v(10, (1,), (), 6)
+        project_v(11, (1,), (), 7)
+        combine(4, 512, 256, ("wv11_1",))
+        combine(5, 0, T, ("wv2_01",))
+        for g in range(GROUPS):
+            project_packed(2, g, (0,), 0 + g)
+        combine(2, 0, T, ("wv3_01",))
+        for g in range(GROUPS):
+            project_packed(2, g, (1,), 3 + g)
+        combine(3, 0, 384, ("wv11_0",))
+        combine(3, 384, 384, ("wv10_0",))

@@ -50,7 +50,7 @@ def tile_moe_qkv_kernel(
             [keep.tile([P, GROUP * PASSES, P], U32, name="wk%d_%d" % (h, g), align_bytes=64) for g in range(GROUPS)]
             for h in range(2)
         ]
-        bias_sb = keep.tile([P, 6, E], F32, name="bias_sb")
+        bias_sb = keep.tile([P, 6, 16], F32, name="bias_sb")
         gate_sb = [keep.tile([P, T], F32, name="gate%d" % r) for r in range(2)]
         y = {}
         banks = [psum.tile([P, GROUP, C], F32, name="bank%d" % b) for b in range(8)]
@@ -67,9 +67,9 @@ def tile_moe_qkv_kernel(
             for r in range(4):
                 nc.sync.dma_start(planes[first + r : P : 32, :, :].bitcast(I32), by_row[r].bitcast(I32))
 
-        def gather_words(g):
-            cols = slice(g * GSLOTS, (g + 1) * GSLOTS)
-            for s in range(PASSES):
+        def gather_words(s):
+            for g in range(GROUPS):
+                cols = slice(g * GSLOTS, (g + 1) * GSLOTS)
                 nc.vector.tensor_copy(xg[s][:, cols], xw[s][:].indirect(offs_sb[:, g * 32 : (g + 1) * 32]))
 
         def gather_scales(g):
@@ -119,47 +119,49 @@ def tile_moe_qkv_kernel(
 
         raw = {}
 
-        def load_wv(e, halves):
+        def load_wv(e, halves, by_pass=False):
             width = P * len(halves)
             t = keep.tile([P, PASSES, 4, width], F32, name="wv%d_%s" % (e, "".join(map(str, halves))), align_bytes=64)
             src = wv[e].rearrange("(s p j) n -> p s j n", p=P, j=4)[:, :, :, halves[0] * P : halves[0] * P + width]
-            if width == N:
+            if width == N and not by_pass:
                 nc.sync.dma_start(t[:].rearrange("p s j n -> p s (j n)"), src.rearrange("p s j n -> p s (j n)"))
             else:
                 for s in range(PASSES):
                     nc.sync.dma_start(t[:, s, :, :], src[:, s, :, :])
             raw[e, halves] = t
 
-        def project_v(e, halves, vector_passes, bank):
+        def project_v(experts, halves, vector_passes, bank):
             width = P * len(halves)
-            t = raw[e, halves]
-            rounded = ring.tile([P, PASSES, width, 4], BF16, name="rounded", bufs=5, align_bytes=64)
-            for s in range(PASSES):
-                dst = rounded[:, s, :, :].rearrange("p (c i) j -> p c j i", i=4)
-                src = t[:, s, :, :].rearrange("p j (c i) -> p c j i", i=4)
-                if s in vector_passes:
-                    nc.vector.tensor_copy(dst, src)
-                else:
-                    nc.scalar.copy(dst, src)
-            codes = ring.tile([P, PASSES, width], U32, name="codes", bufs=5, align_bytes=64)
-            plane = ring.tile([P, PASSES, width], U8, name="plane", bufs=5, align_bytes=64)
+            count = len(experts)
+            rounded = ring.tile([P, count, PASSES, width, 4], BF16, name="rounded", bufs=3, align_bytes=64)
+            for i, e in enumerate(experts):
+                for s in range(PASSES):
+                    dst = rounded[:, i, s, :, :].rearrange("p (c i) j -> p c j i", i=4)
+                    src = raw[e, halves][:, s, :, :].rearrange("p j (c i) -> p c j i", i=4)
+                    if (i, s) in vector_passes:
+                        nc.vector.tensor_copy(dst, src)
+                    else:
+                        nc.scalar.copy(dst, src)
+            codes = ring.tile([P, count, PASSES, width], U32, name="codes", bufs=3, align_bytes=64)
+            plane = ring.tile([P, count, PASSES, width], U8, name="plane", bufs=3, align_bytes=64)
             nc.vector.quantize_mx(
-                codes[:].rearrange("p s n -> p (s n)").bitcast(FP8X4),
-                plane[:].rearrange("p s n -> p (s n)"),
-                rounded[:].rearrange("p s n j -> p (s n j)"),
+                codes[:].rearrange("p e s n -> p (e s n)").bitcast(FP8X4),
+                plane[:].rearrange("p e s n -> p (e s n)"),
+                rounded[:].rearrange("p e s n j -> p (e s n j)"),
             )
-            slots = slice(e * C, (e + 1) * C)
             acc = banks[bank]
-            for i, h in enumerate(halves):
-                cols = slice(i * P, (i + 1) * P)
+            blocks = [(i, e, j, h) for i, e in enumerate(experts) for j, h in enumerate(halves)]
+            for b, (i, e, j, h) in enumerate(blocks):
+                slots = slice(e * C, (e + 1) * C)
+                cols = slice(j * P, (j + 1) * P)
                 for s in range(PASSES):
                     nc.tensor.matmul_mx(
-                        acc[:, i, :], lhsT=codes[:, s, cols].bitcast(FP8X4), lhsT_scale=plane[:, s, cols],
+                        acc[:, b, :], lhsT=codes[:, i, s, cols].bitcast(FP8X4), lhsT_scale=plane[:, i, s, cols],
                         rhs=xg[s][:, slots].bitcast(FP8X4), rhs_scale=xsg[s][:, slots],
                         start=(s == 0), stop=(s == PASSES - 1),
                     )
-            for i, h in enumerate(halves):
-                evacuate(4 + h, e, acc[:, i, :])
+            for b, (i, e, j, h) in enumerate(blocks):
+                evacuate(4 + h, e, acc[:, b, :])
 
         def combine(m, first_token, width, slots):
             cols = slice(first_token, first_token + width)
@@ -176,9 +178,9 @@ def tile_moe_qkv_kernel(
 
         both = (0, 1)
         nc.sync.dma_start(offs_sb[:], offs)
-        for s in range(PASSES):
-            nc.sync.dma_start(xw[s][:].bitcast(I32), x_words[s].rearrange("p t d -> p (t d)").bitcast(I32))
-        load_wv(0, both)
+        nc.sync.dma_start(xw[0][:].bitcast(I32), x_words[0].rearrange("p t d -> p (t d)").bitcast(I32))
+        load_wv(0, both, by_pass=True)
+        nc.sync.dma_start(xw[1][:].bitcast(I32), x_words[1].rearrange("p t d -> p (t d)").bitcast(I32))
         x_by_row = x_scales.rearrange("s (q r) t -> r q s t", r=4)
         for r in range(4):
             nc.sync.dma_start(xs[r:P:32, :, :].bitcast(I32), x_by_row[r].bitcast(I32))
@@ -187,16 +189,23 @@ def tile_moe_qkv_kernel(
         load_wv(3, both)
         load_planes(qplanes, 0, wq_scales)
         load_wq(0)
-        nc.sync.dma_start(bias_sb[:], bias.rearrange("(m p) e -> p m e", p=P))
+        nc.sync.dma_start(bias_sb[:, :, :E], bias.rearrange("(m p) e -> p m e", p=P))
         load_wq(1)
         load_wq(2)
         for r, pos in enumerate((pos1, pos2)):
             nc.sync.dma_start(pos_sb[r][:], pos)
             nc.sync.dma_start(gate_sb[r][:], gate[r])
         load_wv(4, both)
+        load_planes(kplanes, 4, wk_scales)
+        load_wk(0, 0)
         load_wv(5, both)
+        load_wk(0, 1)
+        load_wk(0, 2)
         load_wv(6, both)
+        load_wk(1, 0)
+        load_wk(1, 1)
         load_wv(7, both)
+        load_wk(1, 2)
         load_wv(8, (0,))
         load_wv(9, (0,))
         load_wv(10, (0,))
@@ -205,47 +214,32 @@ def tile_moe_qkv_kernel(
         load_wv(9, (1,))
         load_wv(10, (1,))
         load_wv(11, (1,))
-        load_planes(kplanes, 4, wk_scales)
-        for g in range(GROUPS):
-            load_wk(0, g)
-        for g in range(GROUPS):
-            load_wk(1, g)
 
-        for g in range(GROUPS):
-            gather_words(g)
+        for s in range(PASSES):
+            gather_words(s)
         for g in range(GROUPS):
             gather_scales(g)
         for h in range(2):
             for g in range(GROUPS):
                 project_packed(0, g, (h,), GROUPS * h + g)
-        project_v(0, both, (), 5)
-        project_v(1, both, (), 5)
-        project_v(2, both, (), 5)
-        project_v(3, both, (), 5)
-        combine(0, 0, 384, ("wq0",))
-        combine(0, 384, 384, ("wq1",))
-        project_v(4, both, (), 6)
-        combine(1, 0, 384, ("wv4_01",))
-        project_v(5, both, (), 7)
-        combine(1, 384, 384, ("wv5_01",))
-        project_v(6, both, (1,), 6)
-        project_v(7, both, (1,), 7)
-        project_v(8, (0,), (1,), 6)
-        project_v(9, (0,), (1,), 7)
-        project_v(10, (0,), (1,), 6)
-        project_v(11, (0,), (1,), 7)
-        combine(4, 0, 256, ("wq2",))
-        project_v(8, (1,), (), 6)
-        project_v(9, (1,), (), 7)
-        combine(4, 256, 256, ("wv9_1",))
-        project_v(10, (1,), (), 6)
-        project_v(11, (1,), (), 7)
-        combine(4, 512, 256, ("wv11_1",))
-        combine(5, 0, T, ("wv2_01",))
+        project_v((0, 1), both, (), 5)
+        project_v((2, 3), both, (), 5)
+        combine(0, 0, 768, ("wv3_01",))
+        combine(1, 0, 384, ("wq0",))
+        project_v((4, 5), both, (), 6)
+        combine(1, 384, 384, ("wq1",))
         for g in range(GROUPS):
             project_packed(2, g, (0,), 0 + g)
-        combine(2, 0, T, ("wv3_01",))
+        combine(2, 0, 768, ("wv2_01",))
         for g in range(GROUPS):
             project_packed(2, g, (1,), 3 + g)
-        combine(3, 0, 384, ("wv11_0",))
-        combine(3, 384, 384, ("wv10_0",))
+        combine(3, 0, 768, ("wq2", "xw0"))
+        project_v((6, 7), both, ((0, 1), (1, 1)), 7)
+        project_v((8, 9), (0,), ((1, 1),), 6)
+        project_v((10, 11), (0,), ((0, 1),), 7)
+        combine(4, 0, 384, ("wv11_0",))
+        project_v((8, 9), (1,), ((0, 1), (1, 1)), 6)
+        project_v((10, 11), (1,), (), 7)
+        combine(4, 384, 384, ("wv11_1",))
+        combine(5, 0, 384, ("xw1",))
+        combine(5, 384, 384, ("wv4_01", "wv5_01"))

@@ -1,6 +1,7 @@
 from contextlib import ExitStack
 
 import concourse.mybir as mybir
+from concourse.masks import make_identity
 
 K, T, E, C, N = 1024, 768, 12, 128, 256
 S = E * C
@@ -51,21 +52,38 @@ def tile_moe_qkv_kernel(
             for h in range(2)
         ]
         bias_sb = keep.tile([P, 6, 16], F32, name="bias_sb")
-        gate_sb = [keep.tile([P, T], F32, name="gate%d" % r) for r in range(2)]
+        gate_rows = keep.tile([P, P], F32, name="gate_rows")
+        gate_cols = keep.tile([P, 16], F32, name="gate_cols")
+        identity = keep.tile([P, P], F32, name="identity")
+        gate_sb = keep.tile([P, 2 * T], F32, name="gate_sb")
         y = {}
         banks = [psum.tile([P, GROUP, C], F32, name="bank%d" % b) for b in range(8)]
 
         q_words = qplanes[:].rearrange("p a n -> p (a n)").bitcast(I32)
         half_words = E * PASSES * N // 8
         nc.gpsimd.memset(xs[:].rearrange("p s t -> p (s t)").bitcast(I32), 0)
+        nc.vector.memset(gate_rows[:], 0.0)
         nc.vector.memset(q_words[:, :half_words], 0)
         nc.gpsimd.memset(q_words[:, half_words:], 0)
-        nc.gpsimd.memset(kplanes[:].rearrange("p a n -> p (a n)").bitcast(I32), 0)
+        k_words = kplanes[:].rearrange("p a n -> p (a n)").bitcast(I32)
+        nc.vector.memset(k_words[:, :1024], 0)
+        nc.gpsimd.memset(k_words[:, 1024:], 0)
+        make_identity(nc, identity[:])
 
         def load_planes(planes, first, scales):
             by_row = scales.rearrange("e s (q r) n -> r q (e s) n", r=4)
             for r in range(4):
                 nc.sync.dma_start(planes[first + r : P : 32, :, :].bitcast(I32), by_row[r].bitcast(I32))
+
+        def spread_gate():
+            nc.tensor.transpose(banks[7][:, 0, :], gate_rows[:], identity[:])
+            nc.scalar.copy(gate_cols[:], banks[7][:, 0, :16])
+            for b in range(3):
+                for i in range(GROUP):
+                    r, c = divmod(GROUP * b + i, 6)
+                    column = gate_cols[:, 8 * r + c : 8 * r + c + 1]
+                    nc.tensor.transpose(banks[5 + b][:, i, :], column.to_broadcast([P, P]), identity[:])
+                nc.scalar.copy(gate_sb[:, b * GSLOTS : (b + 1) * GSLOTS], banks[5 + b][:].rearrange("p i c -> p (i c)"))
 
         def gather_words(s):
             for g in range(GROUPS):
@@ -172,7 +190,7 @@ def tile_moe_qkv_kernel(
             else:
                 terms = [keep.tile([P, width], F32, name=slot, align_bytes=64)[:] for slot in slots]
             for r in range(2):
-                nc.vector.tensor_tensor(terms[r], y[m][:].indirect(pos_sb[r][:, lcols]), gate_sb[r][:, cols], MULT)
+                nc.vector.tensor_tensor(terms[r], y[m][:].indirect(pos_sb[r][:, lcols]), gate_sb[:, r * T + first_token : r * T + first_token + width], MULT)
             nc.vector.tensor_tensor(terms[0], terms[0], terms[1], ADD)
             nc.sync.dma_start(out[m * P : (m + 1) * P, cols], terms[0])
 
@@ -181,6 +199,8 @@ def tile_moe_qkv_kernel(
         nc.sync.dma_start(xw[0][:].bitcast(I32), x_words[0].rearrange("p t d -> p (t d)").bitcast(I32))
         load_wv(0, both, by_pass=True)
         nc.sync.dma_start(xw[1][:].bitcast(I32), x_words[1].rearrange("p t d -> p (t d)").bitcast(I32))
+        gate_runs = gate.rearrange("r p t -> r (p t)")[:, : 8 * P].rearrange("r (c j) -> r c j", j=P)
+        nc.sync.dma_start(gate_rows[0:16, :], gate_runs)
         x_by_row = x_scales.rearrange("s (q r) t -> r q s t", r=4)
         for r in range(4):
             nc.sync.dma_start(xs[r:P:32, :, :].bitcast(I32), x_by_row[r].bitcast(I32))
@@ -194,7 +214,6 @@ def tile_moe_qkv_kernel(
         load_wq(2)
         for r, pos in enumerate((pos1, pos2)):
             nc.sync.dma_start(pos_sb[r][:], pos)
-            nc.sync.dma_start(gate_sb[r][:], gate[r])
         load_wv(4, both)
         load_planes(kplanes, 4, wk_scales)
         load_wk(0, 0)
@@ -215,6 +234,7 @@ def tile_moe_qkv_kernel(
         load_wv(10, (1,))
         load_wv(11, (1,))
 
+        spread_gate()
         for s in range(PASSES):
             gather_words(s)
         for g in range(GROUPS):

@@ -18,13 +18,16 @@ FP4X4 = mybir.dt.float4_e2m1fn_x4
 MULT = mybir.AluOpType.mult
 ADD = mybir.AluOpType.add
 IDENTITY = mybir.ActivationFunctionType.Identity
+COPY = mybir.ActivationFunctionType.Copy
 
 P = 128
 PASSES = 2
 GROUP = 4
 GROUPS = E // GROUP
 GSLOTS = GROUP * C
-SPLIT = 4
+RBUFS = 4
+CBUFS = 5
+VFROM = 7
 
 
 def tile_moe_qkv_kernel(
@@ -44,33 +47,24 @@ def tile_moe_qkv_kernel(
         xs = keep.tile([P, PASSES, T], U8, name="xs", align_bytes=64)
         xg = [keep.tile([P, S], U32, name="xg%d" % s, align_bytes=64) for s in range(PASSES)]
         xsg = [keep.tile([P, S], U8, name="xsg%d" % s, align_bytes=64) for s in range(PASSES)]
-        qplanes = keep.tile([P, E * PASSES, N], U8, name="qplanes", align_bytes=64)
-        kplanes = keep.tile([P, E * PASSES, N], U8, name="kplanes", align_bytes=64)
+        planes = keep.tile([P, E * PASSES, N], U8, name="planes", align_bytes=64)
         wq_sb = [keep.tile([P, GROUP * PASSES, 2 * N], U8, name="wq%d" % g, align_bytes=64) for g in range(GROUPS)]
-        wk_sb = [
-            [keep.tile([P, GROUP * PASSES, P], U32, name="wk%d_%d" % (h, g), align_bytes=64) for g in range(GROUPS)]
-            for h in range(2)
-        ]
-        bias_sb = keep.tile([P, 6, 16], F32, name="bias_sb")
+        wk_sb = [keep.tile([P, GROUP * PASSES, N], U32, name="wk%d" % g, align_bytes=64) for g in range(GROUPS)]
+        bias_qk = keep.tile([P, 4, 16], F32, name="bias_qk")
+        bias_v = [keep.tile([P, 2, 8], F32, name="bias_v%d" % g) for g in range(GROUPS)]
         gate_rows = keep.tile([P, P], F32, name="gate_rows")
         gate_cols = keep.tile([P, 16], F32, name="gate_cols")
         identity = keep.tile([P, P], F32, name="identity")
         gate_sb = keep.tile([P, 2 * T], F32, name="gate_sb")
-        y = {}
+        y = [keep.tile([P, S], F32, name="y%d" % m) for m in range(6)]
         banks = [psum.tile([P, GROUP, C], F32, name="bank%d" % b) for b in range(8)]
 
-        q_words = qplanes[:].rearrange("p a n -> p (a n)").bitcast(I32)
-        half_words = E * PASSES * N // 8
         nc.gpsimd.memset(xs[:].rearrange("p s t -> p (s t)").bitcast(I32), 0)
         nc.vector.memset(gate_rows[:], 0.0)
-        nc.vector.memset(q_words[:, :half_words], 0)
-        nc.gpsimd.memset(q_words[:, half_words:], 0)
-        k_words = kplanes[:].rearrange("p a n -> p (a n)").bitcast(I32)
-        nc.vector.memset(k_words[:, :1024], 0)
-        nc.gpsimd.memset(k_words[:, 1024:], 0)
+        nc.vector.memset(planes[:].rearrange("p a n -> p (a n)").bitcast(I32), 0)
         make_identity(nc, identity[:])
 
-        def load_planes(planes, first, scales):
+        def load_planes(first, scales):
             by_row = scales.rearrange("e s (q r) n -> r q (e s) n", r=4)
             for r in range(4):
                 nc.sync.dma_start(planes[first + r : P : 32, :, :].bitcast(I32), by_row[r].bitcast(I32))
@@ -82,8 +76,8 @@ def tile_moe_qkv_kernel(
                 for i in range(GROUP):
                     r, c = divmod(GROUP * b + i, 6)
                     column = gate_cols[:, 8 * r + c : 8 * r + c + 1]
-                    nc.tensor.transpose(banks[5 + b][:, i, :], column.to_broadcast([P, P]), identity[:])
-                nc.scalar.copy(gate_sb[:, b * GSLOTS : (b + 1) * GSLOTS], banks[5 + b][:].rearrange("p i c -> p (i c)"))
+                    nc.tensor.transpose(banks[4 + b][:, i, :], column.to_broadcast([P, P]), identity[:])
+                nc.scalar.copy(gate_sb[:, b * GSLOTS : (b + 1) * GSLOTS], banks[4 + b][:].rearrange("p i c -> p (i c)"))
 
         def gather_words(s):
             for g in range(GROUPS):
@@ -99,167 +93,179 @@ def tile_moe_qkv_kernel(
             src = wq_words[g * GROUP : (g + 1) * GROUP].rearrange("e s p b -> p (e s) b")
             nc.sync.dma_start(wq_sb[g][:].bitcast(I32), src.bitcast(I32))
 
-        def load_wk(h, g):
-            src = wk_words[g * GROUP : (g + 1) * GROUP, :, :, h * P : (h + 1) * P, :].rearrange("e s p n d -> p (e s) (n d)")
-            nc.sync.dma_start(wk_sb[h][g][:].bitcast(I32), src.bitcast(I32))
+        def load_wk(g):
+            src = wk_words[g * GROUP : (g + 1) * GROUP].rearrange("e s p n d -> p (e s) (n d)")
+            nc.sync.dma_start(wk_sb[g][:].bitcast(I32), src.bitcast(I32))
 
-        def y_tile(m):
-            if m not in y:
-                if m in (2, 3):
-                    y[m] = keep.tile([P, S], F32, name="wv%d_01" % (m - 2), align_bytes=64)
-                else:
-                    y[m] = keep.tile([P, S], F32, name="y%d" % m)
-            return y[m]
+        def evacuate(m, e, acc, column):
+            nc.scalar.activation(y[m][:, e * C : (e + 1) * C], acc, IDENTITY, bias=column)
 
-        def evacuate(m, e, acc):
-            nc.scalar.activation(y_tile(m)[:, e * C : (e + 1) * C], acc, IDENTITY, bias=bias_sb[:, m, e : e + 1])
-
-        def project_packed(first_m, g, halves, bank):
-            for h in halves:
-                acc = banks[bank]
-                for i in range(GROUP):
-                    e = g * GROUP + i
-                    slots = slice(e * C, (e + 1) * C)
-                    for s in range(PASSES):
-                        cols = slice(h * P, (h + 1) * P)
-                        if first_m == 0:
-                            lhsT = wq_sb[g][:, i * PASSES + s, 2 * h * P : 2 * (h + 1) * P].bitcast(FP4X4)
-                            lhsT_scale = qplanes[:, e * PASSES + s, cols]
-                        else:
-                            lhsT = wk_sb[h][g][:, i * PASSES + s, :].bitcast(FP8X4)
-                            lhsT_scale = kplanes[4:P, e * PASSES + s, cols]
-                        nc.tensor.matmul_mx(
-                            acc[:, i, :], lhsT=lhsT, lhsT_scale=lhsT_scale, rhs=xg[s][:, slots].bitcast(FP8X4),
-                            rhs_scale=xsg[s][:, slots], start=(s == 0), stop=(s == PASSES - 1),
-                        )
-                for i in range(GROUP):
-                    evacuate(first_m + h, g * GROUP + i, acc[:, i, :])
+        def project_packed(first_m, g, h, bank):
+            acc = banks[bank]
+            cols = slice(h * P, (h + 1) * P)
+            for i in range(GROUP):
+                e = g * GROUP + i
+                slots = slice(e * C, (e + 1) * C)
+                for s in range(PASSES):
+                    if first_m == 0:
+                        lhsT = wq_sb[g][:, i * PASSES + s, 2 * h * P : 2 * (h + 1) * P].bitcast(FP4X4)
+                        lhsT_scale = planes[:, e * PASSES + s, cols]
+                    else:
+                        lhsT = wk_sb[g][:, i * PASSES + s, cols].bitcast(FP8X4)
+                        lhsT_scale = planes[4:P, e * PASSES + s, cols]
+                    nc.tensor.matmul_mx(
+                        acc[:, i, :], lhsT=lhsT, lhsT_scale=lhsT_scale, rhs=xg[s][:, slots].bitcast(FP8X4),
+                        rhs_scale=xsg[s][:, slots], start=(s == 0), stop=(s == PASSES - 1),
+                    )
+            for i in range(GROUP):
+                e = g * GROUP + i
+                evacuate(first_m + h, e, acc[:, i, :], bias_qk[:, first_m + h, e : e + 1])
 
         raw = {}
 
-        def load_wv(e, halves, by_pass=False):
-            width = P * len(halves)
-            t = keep.tile([P, PASSES, 4, width], F32, name="wv%d_%s" % (e, "".join(map(str, halves))), align_bytes=64)
-            src = wv[e].rearrange("(s p j) n -> p s j n", p=P, j=4)[:, :, :, halves[0] * P : halves[0] * P + width]
-            if width == N and not by_pass:
-                nc.sync.dma_start(t[:].rearrange("p s j n -> p s (j n)"), src.rearrange("p s j n -> p s (j n)"))
+        def load_wv(e, by_pass=False):
+            raw[e] = keep.tile([P, PASSES, 4, N], F32, name="wv%d" % e, align_bytes=64)
+            src = wv[e].rearrange("(s p j) n -> p s (j n)", p=P, j=4)
+            dst = raw[e][:].rearrange("p s j n -> p s (j n)")
+            if by_pass:
+                for s in range(PASSES):
+                    nc.sync.dma_start(dst[:, s, :], src[:, s, :])
             else:
-                for s in range(PASSES):
-                    nc.sync.dma_start(t[:, s, :, :], src[:, s, :, :])
-            raw[e, halves] = t
+                nc.sync.dma_start(dst, src)
 
-        def project_v(experts, halves, vector_passes, bank):
-            width = P * len(halves)
-            count = len(experts)
-            rounded = ring.tile([P, count, PASSES, width, 4], BF16, name="rounded", bufs=3, align_bytes=64)
-            for i, e in enumerate(experts):
-                for s in range(PASSES):
-                    dst = rounded[:, i, s, :, :].rearrange("p (c i) j -> p c j i", i=4)
-                    src = raw[e, halves][:, s, :, :].rearrange("p j (c i) -> p c j i", i=4)
-                    if (i, s) in vector_passes:
-                        nc.vector.tensor_copy(dst, src)
-                    else:
-                        nc.scalar.copy(dst, src)
-            codes = ring.tile([P, count, PASSES, width], U32, name="codes", bufs=3, align_bytes=64)
-            plane = ring.tile([P, count, PASSES, width], U8, name="plane", bufs=3, align_bytes=64)
-            nc.vector.quantize_mx(
-                codes[:].rearrange("p e s n -> p (e s n)").bitcast(FP8X4),
-                plane[:].rearrange("p e s n -> p (e s n)"),
-                rounded[:].rearrange("p e s n j -> p (e s n j)"),
-            )
-            acc = banks[bank]
-            blocks = [(i, e, j, h) for i, e in enumerate(experts) for j, h in enumerate(halves)]
-            for b, (i, e, j, h) in enumerate(blocks):
-                slots = slice(e * C, (e + 1) * C)
-                cols = slice(j * P, (j + 1) * P)
+        rounded_of = {}
+
+        def round_v(e, vector_passes):
+            rounded = ring.tile([P, PASSES, N, 4], BF16, name="rounded", bufs=RBUFS, align_bytes=64)
+            for s in range(PASSES):
+                dst = rounded[:, s, :, :].rearrange("p (c i) j -> p c j i", i=4)
+                src = raw[e][:, s, :, :].rearrange("p j (c i) -> p c j i", i=4)
+                if s in vector_passes:
+                    nc.vector.tensor_copy(dst, src)
+                else:
+                    nc.scalar.copy(dst, src)
+            rounded_of[e] = rounded
+
+        quantised = {}
+
+        def quantise_v(e, by_pass=False):
+            rounded = rounded_of[e]
+            codes = ring.tile([P, PASSES, N], U32, name="codes", bufs=CBUFS, align_bytes=64)
+            plane = ring.tile([P, PASSES, N], U8, name="plane", bufs=CBUFS, align_bytes=64)
+            for passes in [slice(s, s + 1) for s in range(PASSES)] if by_pass else [slice(0, PASSES)]:
+                nc.vector.quantize_mx(
+                    codes[:, passes, :].rearrange("p s n -> p (s n)").bitcast(FP8X4),
+                    plane[:, passes, :].rearrange("p s n -> p (s n)"),
+                    rounded[:, passes, :, :].rearrange("p s n j -> p (s n j)"),
+                )
+            quantised[e] = (codes, plane)
+
+        def project_v(e):
+            codes, plane = quantised[e]
+            accs = v_accs(e)
+            slots = slice(e * C, (e + 1) * C)
+            for h in range(2):
+                cols = slice(h * P, (h + 1) * P)
                 for s in range(PASSES):
                     nc.tensor.matmul_mx(
-                        acc[:, b, :], lhsT=codes[:, i, s, cols].bitcast(FP8X4), lhsT_scale=plane[:, i, s, cols],
+                        accs[h], lhsT=codes[:, s, cols].bitcast(FP8X4), lhsT_scale=plane[:, s, cols],
                         rhs=xg[s][:, slots].bitcast(FP8X4), rhs_scale=xsg[s][:, slots],
                         start=(s == 0), stop=(s == PASSES - 1),
                     )
-            for b, (i, e, j, h) in enumerate(blocks):
-                evacuate(4 + h, e, acc[:, b, :])
 
-        def combine(m, first_token, width, slots):
+        def v_accs(e):
+            if e == E - 1:
+                return [banks[4][:, h, :] for h in range(2)]
+            return [banks[(6 + 2 * (e // GROUP) + h) % 8][:, e % GROUP, :] for h in range(2)]
+
+        def evacuate_v(experts):
+            for h in range(2):
+                for e in experts:
+                    evacuate(4 + h, e, v_accs(e)[h], bias_v[e // GROUP][:, h, e % GROUP : e % GROUP + 1])
+
+        def combine(m, first_token, width, slot):
             cols = slice(first_token, first_token + width)
             lcols = slice(first_token // 16, (first_token + width) // 16)
-            if len(slots) == 1:
-                pair = keep.tile([P, 2, width], F32, name=slots[0], align_bytes=64)
-                terms = [pair[:, r, :] for r in range(2)]
-            else:
-                terms = [keep.tile([P, width], F32, name=slot, align_bytes=64)[:] for slot in slots]
+            pair = keep.tile([P, 2, width], F32, name=slot, align_bytes=64)
             for r in range(2):
-                nc.vector.tensor_tensor(terms[r], y[m][:].indirect(pos_sb[r][:, lcols]), gate_sb[:, r * T + first_token : r * T + first_token + width], MULT)
-            nc.vector.tensor_tensor(terms[0], terms[0], terms[1], ADD)
-            nc.sync.dma_start(out[m * P : (m + 1) * P, cols], terms[0])
+                weights = gate_sb[:, r * T + first_token : r * T + first_token + width]
+                nc.vector.tensor_tensor(pair[:, r, :], y[m][:].indirect(pos_sb[r][:, lcols]), weights, MULT)
+            nc.vector.tensor_tensor(pair[:, 0, :], pair[:, 0, :], pair[:, 1, :], ADD)
+            nc.sync.dma_start(out[m * P : (m + 1) * P, cols], pair[:, 0, :])
 
-        both = (0, 1)
+        def load_x(s):
+            nc.sync.dma_start(xw[s][:].bitcast(I32), x_words[s].rearrange("p t d -> p (t d)").bitcast(I32))
+
+        def load_x_scales():
+            x_by_row = x_scales.rearrange("s (q r) t -> r q s t", r=4)
+            for r in range(4):
+                nc.sync.dma_start(xs[r:P:32, :, :].bitcast(I32), x_by_row[r].bitcast(I32))
+
+        def load_gate():
+            gate_runs = gate.rearrange("r p t -> r (p t)")[:, : 8 * P].rearrange("r (c j) -> r c j", j=P)
+            nc.sync.dma_start(gate_rows[0:16, :], gate_runs)
+
+        bias_rows = bias.rearrange("(m p) e -> p m e", p=P)
+
+        def load_small():
+            nc.sync.dma_start(bias_qk[:, :, :E], bias_rows[:, :4, :])
+            for r, pos in enumerate((pos1, pos2)):
+                nc.sync.dma_start(pos_sb[r][:], pos)
+
+        def load_bias_v(g):
+            nc.sync.dma_start(bias_v[g][:, :, :GROUP], bias_rows[:, 4:, g * GROUP : (g + 1) * GROUP])
+
         nc.sync.dma_start(offs_sb[:], offs)
-        nc.sync.dma_start(xw[0][:].bitcast(I32), x_words[0].rearrange("p t d -> p (t d)").bitcast(I32))
-        load_wv(0, both, by_pass=True)
-        nc.sync.dma_start(xw[1][:].bitcast(I32), x_words[1].rearrange("p t d -> p (t d)").bitcast(I32))
-        gate_runs = gate.rearrange("r p t -> r (p t)")[:, : 8 * P].rearrange("r (c j) -> r c j", j=P)
-        nc.sync.dma_start(gate_rows[0:16, :], gate_runs)
-        x_by_row = x_scales.rearrange("s (q r) t -> r q s t", r=4)
-        for r in range(4):
-            nc.sync.dma_start(xs[r:P:32, :, :].bitcast(I32), x_by_row[r].bitcast(I32))
-        load_wv(1, both)
-        load_wv(2, both)
-        load_wv(3, both)
-        load_planes(qplanes, 0, wq_scales)
+        load_x(0)
+        load_x(1)
+        load_wv(0)
+        load_gate()
+        load_x_scales()
+        load_planes(0, wq_scales)
+        load_planes(4, wk_scales)
         load_wq(0)
-        nc.sync.dma_start(bias_sb[:, :, :E], bias.rearrange("(m p) e -> p m e", p=P))
+        load_small()
         load_wq(1)
         load_wq(2)
-        for r, pos in enumerate((pos1, pos2)):
-            nc.sync.dma_start(pos_sb[r][:], pos)
-        load_wv(4, both)
-        load_planes(kplanes, 4, wk_scales)
-        load_wk(0, 0)
-        load_wv(5, both)
-        load_wk(0, 1)
-        load_wk(0, 2)
-        load_wv(6, both)
-        load_wk(1, 0)
-        load_wk(1, 1)
-        load_wv(7, both)
-        load_wk(1, 2)
-        load_wv(8, (0,))
-        load_wv(9, (0,))
-        load_wv(10, (0,))
-        load_wv(11, (0,))
-        load_wv(8, (1,))
-        load_wv(9, (1,))
-        load_wv(10, (1,))
-        load_wv(11, (1,))
+        load_wv(1)
+        for g in range(GROUPS):
+            load_wk(g)
+        for e in range(2, E):
+            load_wv(e, by_pass=e == E - 1)
+            if e in (5, 9, 10):
+                load_bias_v((5, 9, 10).index(e))
 
         spread_gate()
         for s in range(PASSES):
             gather_words(s)
         for g in range(GROUPS):
             gather_scales(g)
-        for h in range(2):
-            for g in range(GROUPS):
-                project_packed(0, g, (h,), GROUPS * h + g)
-        project_v((0, 1), both, (), 5)
-        project_v((2, 3), both, (), 5)
-        combine(0, 0, 768, ("wv3_01",))
-        combine(1, 0, 384, ("wq0",))
-        project_v((4, 5), both, (), 6)
-        combine(1, 384, 384, ("wq1",))
+        round_v(0, ())
         for g in range(GROUPS):
-            project_packed(2, g, (0,), 0 + g)
-        combine(2, 0, 768, ("wv2_01",))
+            for h in range(2):
+                project_packed(0, g, h, 2 + 2 * g + h)
+        round_v(1, ())
+        combine(0, 0, T, "wv0")
+        quantise_v(0)
+        combine(1, 0, T, "xw0")
+        quantise_v(1)
         for g in range(GROUPS):
-            project_packed(2, g, (1,), 3 + g)
-        combine(3, 0, 768, ("wq2", "xw0"))
-        project_v((6, 7), both, ((0, 1), (1, 1)), 7)
-        project_v((8, 9), (0,), ((1, 1),), 6)
-        project_v((10, 11), (0,), ((0, 1),), 7)
-        combine(4, 0, 384, ("wv11_0",))
-        project_v((8, 9), (1,), ((0, 1), (1, 1)), 6)
-        project_v((10, 11), (1,), (), 7)
-        combine(4, 384, 384, ("wv11_1",))
-        combine(5, 0, 384, ("xw1",))
-        combine(5, 384, 384, ("wv4_01", "wv5_01"))
+            for h in range(2):
+                project_packed(2, g, h, 2 + 2 * g + h)
+        for e in range(2):
+            project_v(e)
+        for e in range(2, E):
+            round_v(e, (1,) if e >= VFROM else ())
+            quantise_v(e, by_pass=e == E - 1)
+            project_v(e)
+            if e in (2, 3, 4, 5):
+                combine(2 + (e - 2) // 2, (e % 2) * T // 2, T // 2, "wv%d" % (e - 1))
+            if e == 5:
+                evacuate_v(range(0, 4))
+            if e == 9:
+                evacuate_v(range(4, 8))
+        evacuate_v(range(8, 11))
+        evacuate_v((11,))
+        combine(4, 0, T, "wv7")
+        combine(5, 0, T // 2, "wv8")
+        combine(5, T // 2, T // 2, "wv9")

@@ -26,8 +26,7 @@ GROUP = 4
 GROUPS = E // GROUP
 GSLOTS = GROUP * C
 RBUFS = 4
-CBUFS = 5
-VFROM = 7
+CBUFS = 4
 
 
 def tile_moe_qkv_kernel(
@@ -84,10 +83,9 @@ def tile_moe_qkv_kernel(
                 cols = slice(g * GSLOTS, (g + 1) * GSLOTS)
                 nc.vector.tensor_copy(xg[s][:, cols], xw[s][:].indirect(offs_sb[:, g * 32 : (g + 1) * 32]))
 
-        def gather_scales(g):
-            cols = slice(g * GSLOTS, (g + 1) * GSLOTS)
+        def gather_scales(first, last):
             for s in range(PASSES):
-                nc.vector.tensor_copy(xsg[s][:, cols], xs[:, s, :].indirect(offs_sb[:, g * 32 : (g + 1) * 32]))
+                nc.vector.tensor_copy(xsg[s][:, first:last], xs[:, s, :].indirect(offs_sb[:, first // 16 : last // 16]))
 
         def load_wq(g):
             src = wq_words[g * GROUP : (g + 1) * GROUP].rearrange("e s p b -> p (e s) b")
@@ -100,10 +98,10 @@ def tile_moe_qkv_kernel(
         def evacuate(m, e, acc, column):
             nc.scalar.activation(y[m][:, e * C : (e + 1) * C], acc, IDENTITY, bias=column)
 
-        def project_packed(first_m, g, h, bank):
+        def project_packed(first_m, g, h, bank, members=range(GROUP)):
             acc = banks[bank]
             cols = slice(h * P, (h + 1) * P)
-            for i in range(GROUP):
+            for i in members:
                 e = g * GROUP + i
                 slots = slice(e * C, (e + 1) * C)
                 for s in range(PASSES):
@@ -117,7 +115,7 @@ def tile_moe_qkv_kernel(
                         acc[:, i, :], lhsT=lhsT, lhsT_scale=lhsT_scale, rhs=xg[s][:, slots].bitcast(FP8X4),
                         rhs_scale=xsg[s][:, slots], start=(s == 0), stop=(s == PASSES - 1),
                     )
-            for i in range(GROUP):
+            for i in members:
                 e = g * GROUP + i
                 evacuate(first_m + h, e, acc[:, i, :], bias_qk[:, first_m + h, e : e + 1])
 
@@ -133,14 +131,44 @@ def tile_moe_qkv_kernel(
             else:
                 nc.sync.dma_start(dst, src)
 
-        rounded_of = {}
+        def load_wv_half(e, h):
+            raw[e, h] = keep.tile([P, PASSES, 4, P], F32, name="wv%d%s" % (e, "b" * h), align_bytes=64)
+            src = wv[e].rearrange("(s p j) n -> p s j n", p=P, j=4)
+            for s in range(PASSES):
+                nc.sync.dma_start(raw[e, h][:, s, :, :], src[:, s, :, h * P : (h + 1) * P])
 
-        def round_v(e, vector_passes):
-            rounded = ring.tile([P, PASSES, N, 4], BF16, name="rounded", bufs=RBUFS, align_bytes=64)
+        def project_v_half(e, h, vector_passes):
+            rounded = ring.tile([P, PASSES, P, 4], BF16, name="rounded", bufs=RBUFS, align_bytes=64)
             for s in range(PASSES):
                 dst = rounded[:, s, :, :].rearrange("p (c i) j -> p c j i", i=4)
-                src = raw[e][:, s, :, :].rearrange("p j (c i) -> p c j i", i=4)
+                src = raw[e, h][:, s, :, :].rearrange("p j (c i) -> p c j i", i=4)
                 if s in vector_passes:
+                    nc.vector.tensor_copy(dst, src)
+                else:
+                    nc.scalar.copy(dst, src)
+            codes = ring.tile([P, PASSES, P], U32, name="codes", bufs=CBUFS, align_bytes=64)
+            plane = ring.tile([P, PASSES, P], U8, name="plane", bufs=CBUFS, align_bytes=64)
+            nc.vector.quantize_mx(
+                codes[:].rearrange("p s n -> p (s n)").bitcast(FP8X4),
+                plane[:].rearrange("p s n -> p (s n)"),
+                rounded[:].rearrange("p s n j -> p (s n j)"),
+            )
+            slots = slice(e * C, (e + 1) * C)
+            for s in range(PASSES):
+                nc.tensor.matmul_mx(
+                    v_accs(e)[h], lhsT=codes[:, s, :].bitcast(FP8X4), lhsT_scale=plane[:, s, :],
+                    rhs=xg[s][:, slots].bitcast(FP8X4), rhs_scale=xsg[s][:, slots],
+                    start=(s == 0), stop=(s == PASSES - 1),
+                )
+
+        rounded_of = {}
+
+        def round_v(e, pieces):
+            rounded = ring.tile([P, PASSES, N, 4], BF16, name="rounded", bufs=RBUFS, align_bytes=64)
+            for s, cols, on_vector in pieces:
+                dst = rounded[:, s, cols, :].rearrange("p (c i) j -> p c j i", i=4)
+                src = raw[e][:, s, :, cols].rearrange("p j (c i) -> p c j i", i=4)
+                if on_vector:
                     nc.vector.tensor_copy(dst, src)
                 else:
                     nc.scalar.copy(dst, src)
@@ -148,15 +176,19 @@ def tile_moe_qkv_kernel(
 
         quantised = {}
 
-        def quantise_v(e, by_pass=False):
+        def quantise_v(e, spans):
             rounded = rounded_of[e]
-            codes = ring.tile([P, PASSES, N], U32, name="codes", bufs=CBUFS, align_bytes=64)
+            if e == 0:
+                codes = keep.tile([P, PASSES, N], U32, name="xs", align_bytes=64)
+            else:
+                codes = ring.tile([P, PASSES, N], U32, name="codes", bufs=CBUFS, align_bytes=64)
             plane = ring.tile([P, PASSES, N], U8, name="plane", bufs=CBUFS, align_bytes=64)
-            for passes in [slice(s, s + 1) for s in range(PASSES)] if by_pass else [slice(0, PASSES)]:
+            code_row = codes[:].rearrange("p s n -> p (s n)")
+            plane_row = plane[:].rearrange("p s n -> p (s n)")
+            value_row = rounded[:].rearrange("p s n j -> p (s n j)")
+            for first, last in spans:
                 nc.vector.quantize_mx(
-                    codes[:, passes, :].rearrange("p s n -> p (s n)").bitcast(FP8X4),
-                    plane[:, passes, :].rearrange("p s n -> p (s n)"),
-                    rounded[:, passes, :, :].rearrange("p s n j -> p (s n j)"),
+                    code_row[:, first:last].bitcast(FP8X4), plane_row[:, first:last], value_row[:, 4 * first : 4 * last]
                 )
             quantised[e] = (codes, plane)
 
@@ -175,11 +207,11 @@ def tile_moe_qkv_kernel(
 
         def v_accs(e):
             if e == E - 1:
-                return [banks[4][:, h, :] for h in range(2)]
+                return [banks[4 + h][:, 0, :] for h in range(2)]
             return [banks[(6 + 2 * (e // GROUP) + h) % 8][:, e % GROUP, :] for h in range(2)]
 
-        def evacuate_v(experts):
-            for h in range(2):
+        def evacuate_v(experts, halves=(0, 1)):
+            for h in halves:
                 for e in experts:
                     evacuate(4 + h, e, v_accs(e)[h], bias_v[e // GROUP][:, h, e % GROUP : e % GROUP + 1])
 
@@ -192,6 +224,26 @@ def tile_moe_qkv_kernel(
                 nc.vector.tensor_tensor(pair[:, r, :], y[m][:].indirect(pos_sb[r][:, lcols]), weights, MULT)
             nc.vector.tensor_tensor(pair[:, 0, :], pair[:, 0, :], pair[:, 1, :], ADD)
             nc.sync.dma_start(out[m * P : (m + 1) * P, cols], pair[:, 0, :])
+
+        def combine_on_tensor(m, first_token, width, slot, sum_bank, back_bank):
+            cols = slice(first_token, first_token + width)
+            lcols = slice(first_token // 16, (first_token + width) // 16)
+            chunks = width // P
+            trio = keep.tile([P, 3, width], F32, name=slot, align_bytes=64)
+            for r in range(2):
+                weights = gate_sb[:, r * T + first_token : r * T + first_token + width]
+                nc.vector.tensor_tensor(trio[:, r, :], y[m][:].indirect(pos_sb[r][:, lcols]), weights, MULT)
+            for c in range(chunks):
+                for r in range(2):
+                    nc.tensor.matmul(
+                        banks[sum_bank][:, c, :], lhsT=trio[:, r, c * P : (c + 1) * P], rhs=identity[:],
+                        is_transpose=True, start=(r == 0), stop=(r == 1),
+                    )
+            nc.scalar.copy(trio[:, 2, :], banks[sum_bank][:, :chunks, :].rearrange("p c n -> p (c n)"))
+            for c in range(chunks):
+                nc.tensor.transpose(banks[back_bank][:, c, :], trio[:, 2, c * P : (c + 1) * P], identity[:])
+            nc.scalar.copy(trio[:, 0, :], banks[back_bank][:, :chunks, :].rearrange("p c n -> p (c n)"))
+            nc.scalar.dma_start(out[m * P : (m + 1) * P, cols], trio[:, 0, :])
 
         def load_x(s):
             nc.sync.dma_start(xw[s][:].bitcast(I32), x_words[s].rearrange("p t d -> p (t d)").bitcast(I32))
@@ -215,6 +267,13 @@ def tile_moe_qkv_kernel(
         def load_bias_v(g):
             nc.sync.dma_start(bias_v[g][:, :, :GROUP], bias_rows[:, 4:, g * GROUP : (g + 1) * GROUP])
 
+        whole, low, high = slice(0, N), slice(0, P), slice(P, N)
+        on_scalar = [(0, whole, False), (1, whole, False)]
+        shared = [(0, whole, False), (1, whole, True)]
+        finest = [(0, whole, False), (1, low, True), (1, high, False)]
+        at_once = [(0, 2 * N)]
+        in_three = [(0, N), (N, N + P), (N + P, 2 * N)]
+
         nc.sync.dma_start(offs_sb[:], offs)
         load_x(0)
         load_x(1)
@@ -228,44 +287,68 @@ def tile_moe_qkv_kernel(
         load_wq(1)
         load_wq(2)
         load_wv(1)
-        for g in range(GROUPS):
-            load_wk(g)
-        for e in range(2, E):
-            load_wv(e, by_pass=e == E - 1)
-            if e in (5, 9, 10):
-                load_bias_v((5, 9, 10).index(e))
+        load_wk(0)
+        load_wk(1)
+        load_wk(2)
+        load_wv(2)
+        load_wv(3)
+        load_wv(4)
+        load_wv(5)
+        load_bias_v(0)
+        load_wv(6)
+        load_wv(7)
+        load_wv(8)
+        load_wv(9)
+        load_bias_v(1)
+        load_wv_half(10, 0)
+        load_wv_half(11, 0)
+        load_bias_v(2)
+        load_wv_half(10, 1)
+        load_wv_half(11, 1)
 
         spread_gate()
         for s in range(PASSES):
             gather_words(s)
-        for g in range(GROUPS):
-            gather_scales(g)
-        round_v(0, ())
-        for g in range(GROUPS):
+        for first, last in ((0, 4), (4, 8), (8, 10), (10, 12)):
+            gather_scales(first * C, last * C)
+        round_v(0, on_scalar)
+        for g in range(GROUPS - 1):
             for h in range(2):
                 project_packed(0, g, h, 2 + 2 * g + h)
-        round_v(1, ())
+        for h in range(2):
+            project_packed(0, 2, h, 6 + h, (0, 1))
+            project_packed(0, 2, h, h, (2, 3))
+        for e in range(1, 2):
+            round_v(e, on_scalar)
+        quantise_v(0, at_once)
         combine(0, 0, T, "wv0")
-        quantise_v(0)
+        for e in range(1, 2):
+            quantise_v(e, at_once)
         combine(1, 0, T, "xw0")
-        quantise_v(1)
         for g in range(GROUPS):
             for h in range(2):
                 project_packed(2, g, h, 2 + 2 * g + h)
         for e in range(2):
             project_v(e)
-        for e in range(2, E):
-            round_v(e, (1,) if e >= VFROM else ())
-            quantise_v(e, by_pass=e == E - 1)
+        for e in range(2, 10):
+            round_v(e, shared if e >= 7 else on_scalar)
+            quantise_v(e, at_once)
             project_v(e)
-            if e in (2, 3, 4, 5):
-                combine(2 + (e - 2) // 2, (e % 2) * T // 2, T // 2, "wv%d" % (e - 1))
+            if e < 2 + 4:
+                combine(2 + (e - 2) // 2, ((e - 2) % 2) * T // 2, T // 2, "wv%d" % (e - 1))
             if e == 5:
                 evacuate_v(range(0, 4))
             if e == 9:
                 evacuate_v(range(4, 8))
-        evacuate_v(range(8, 11))
-        evacuate_v((11,))
-        combine(4, 0, T, "wv7")
-        combine(5, 0, T // 2, "wv8")
-        combine(5, T // 2, T // 2, "wv9")
+        for e in range(10, E):
+            project_v_half(e, 0, (1,))
+        evacuate_v(range(8, 11), (0,))
+        evacuate_v((11,), (0,))
+        for e in range(10, E):
+            project_v_half(e, 1, (1,))
+        evacuate_v(range(8, 11), (1,))
+        evacuate_v((11,), (1,))
+        combine_on_tensor(4, 0, T // 2, "wv5", 6, 7)
+        combine_on_tensor(4, T // 2, T // 2, "wv6", 0, 1)
+        combine(5, 0, 512, "wv0")
+        combine(5, 512, 256, "wv1")

@@ -25,6 +25,7 @@ PASSES = 2
 GROUP = 4
 GROUPS = E // GROUP
 GSLOTS = GROUP * C
+RUN = 96
 RBUFS = 4
 CBUFS = 4
 
@@ -71,12 +72,12 @@ def tile_moe_qkv_kernel(
         def spread_gate():
             nc.tensor.transpose(banks[7][:, 0, :], gate_rows[:], identity[:])
             nc.scalar.copy(gate_cols[:], banks[7][:, 0, :16])
-            for b in range(3):
+            for b in range(4):
                 for i in range(GROUP):
-                    r, c = divmod(GROUP * b + i, 6)
-                    column = gate_cols[:, 8 * r + c : 8 * r + c + 1]
-                    nc.tensor.transpose(banks[4 + b][:, i, :], column.to_broadcast([P, P]), identity[:])
-                nc.scalar.copy(gate_sb[:, b * GSLOTS : (b + 1) * GSLOTS], banks[4 + b][:].rearrange("p i c -> p (i c)"))
+                    column = gate_cols[:, GROUP * b + i : GROUP * b + i + 1]
+                    nc.tensor.transpose(banks[3 + b][:, i, :], column.to_broadcast([P, P]), identity[:])
+                runs = gate_sb[:, b * GROUP * RUN : (b + 1) * GROUP * RUN].rearrange("p (i j) -> p i j", j=RUN)
+                nc.scalar.copy(runs, banks[3 + b][:, :, :RUN])
 
         def gather_words(s):
             for g in range(GROUPS):
@@ -140,8 +141,9 @@ def tile_moe_qkv_kernel(
         def project_v_half(e, h, vector_passes):
             rounded = ring.tile([P, PASSES, P, 4], BF16, name="rounded", bufs=RBUFS, align_bytes=64)
             for s in range(PASSES):
-                dst = rounded[:, s, :, :].rearrange("p (c i) j -> p c j i", i=4)
-                src = raw[e, h][:, s, :, :].rearrange("p j (c i) -> p c j i", i=4)
+                run = 2 if s in vector_passes else 4
+                dst = rounded[:, s, :, :].rearrange("p (c i) j -> p c j i", i=run)
+                src = raw[e, h][:, s, :, :].rearrange("p j (c i) -> p c j i", i=run)
                 if s in vector_passes:
                     nc.vector.tensor_copy(dst, src)
                 else:
@@ -166,8 +168,9 @@ def tile_moe_qkv_kernel(
         def round_v(e, pieces):
             rounded = ring.tile([P, PASSES, N, 4], BF16, name="rounded", bufs=RBUFS, align_bytes=64)
             for s, cols, on_vector in pieces:
-                dst = rounded[:, s, cols, :].rearrange("p (c i) j -> p c j i", i=4)
-                src = raw[e][:, s, :, cols].rearrange("p j (c i) -> p c j i", i=4)
+                run = 2 if on_vector else 4
+                dst = rounded[:, s, cols, :].rearrange("p (c i) j -> p c j i", i=run)
+                src = raw[e][:, s, :, cols].rearrange("p j (c i) -> p c j i", i=run)
                 if on_vector:
                     nc.vector.tensor_copy(dst, src)
                 else:
@@ -254,8 +257,7 @@ def tile_moe_qkv_kernel(
                 nc.sync.dma_start(xs[r:P:32, :, :].bitcast(I32), x_by_row[r].bitcast(I32))
 
         def load_gate():
-            gate_runs = gate.rearrange("r p t -> r (p t)")[:, : 8 * P].rearrange("r (c j) -> r c j", j=P)
-            nc.sync.dma_start(gate_rows[0:16, :], gate_runs)
+            nc.sync.dma_start(gate_rows[0:16, :RUN], gate[:, 0, :].rearrange("r (c j) -> r c j", j=RUN))
 
         bias_rows = bias.rearrange("(m p) e -> p m e", p=P)
 

@@ -26,8 +26,9 @@ GROUP = 4
 GROUPS = E // GROUP
 GSLOTS = GROUP * C
 RUN = 96
-RBUFS = 4
+RBUFS = 7
 CBUFS = 4
+SHARED_FROM = 4
 
 
 def tile_moe_qkv_kernel(
@@ -44,14 +45,13 @@ def tile_moe_qkv_kernel(
         pos_sb = [lists.tile([P, T // 16], U16, name="pos%d_sb" % r) for r in range(2)]
 
         xw = [keep.tile([P, T], U32, name="xw%d" % s, align_bytes=64) for s in range(PASSES)]
-        xs = keep.tile([P, PASSES, T], U8, name="xs", align_bytes=64)
+        xs = keep.tile([P, T], U8, name="xs", align_bytes=64)
         xg = [keep.tile([P, S], U32, name="xg%d" % s, align_bytes=64) for s in range(PASSES)]
-        xsg = [keep.tile([P, S], U8, name="xsg%d" % s, align_bytes=64) for s in range(PASSES)]
+        xsg = keep.tile([P, S], U8, name="xsg", align_bytes=64)
+        xsg_moved = keep.tile([P, S], U8, name="xsg_moved", align_bytes=64)
         planes = keep.tile([P, E * PASSES, N], U8, name="planes", align_bytes=64)
         wq_sb = [keep.tile([P, GROUP * PASSES, 2 * N], U8, name="wq%d" % g, align_bytes=64) for g in range(GROUPS)]
-        wk_sb = [keep.tile([P, GROUP * PASSES, N], U32, name="wk%d" % g, align_bytes=64) for g in range(GROUPS)]
-        bias_qk = keep.tile([P, 4, 16], F32, name="bias_qk")
-        bias_v = [keep.tile([P, 2, 8], F32, name="bias_v%d" % g) for g in range(GROUPS)]
+        bias_sb = keep.tile([P, 6, 16], F32, name="bias_sb")
         gate_rows = keep.tile([P, P], F32, name="gate_rows")
         gate_cols = keep.tile([P, 16], F32, name="gate_cols")
         identity = keep.tile([P, P], F32, name="identity")
@@ -59,7 +59,8 @@ def tile_moe_qkv_kernel(
         y = [keep.tile([P, S], F32, name="y%d" % m) for m in range(6)]
         banks = [psum.tile([P, GROUP, C], F32, name="bank%d" % b) for b in range(8)]
 
-        nc.gpsimd.memset(xs[:].rearrange("p s t -> p (s t)").bitcast(I32), 0)
+        nc.gpsimd.memset(xs[:].bitcast(I32), 0)
+        nc.gpsimd.memset(xsg_moved[:].bitcast(I32), 0)
         nc.vector.memset(gate_rows[:], 0.0)
         nc.vector.memset(planes[:].rearrange("p a n -> p (a n)").bitcast(I32), 0)
         make_identity(nc, identity[:])
@@ -79,46 +80,58 @@ def tile_moe_qkv_kernel(
                 runs = gate_sb[:, b * GROUP * RUN : (b + 1) * GROUP * RUN].rearrange("p (i j) -> p i j", j=RUN)
                 nc.scalar.copy(runs, banks[3 + b][:, :, :RUN])
 
-        def gather_words(s):
-            for g in range(GROUPS):
-                cols = slice(g * GSLOTS, (g + 1) * GSLOTS)
-                nc.vector.tensor_copy(xg[s][:, cols], xw[s][:].indirect(offs_sb[:, g * 32 : (g + 1) * 32]))
+        def gather_words(s, g):
+            cols = slice(g * GSLOTS, (g + 1) * GSLOTS)
+            nc.vector.tensor_copy(xg[s][:, cols], xw[s][:].indirect(offs_sb[:, g * 32 : (g + 1) * 32]))
 
-        def gather_scales(first, last):
-            for s in range(PASSES):
-                nc.vector.tensor_copy(xsg[s][:, first:last], xs[:, s, :].indirect(offs_sb[:, first // 16 : last // 16]))
+        def gather_scales(g):
+            cols = slice(g * GSLOTS, (g + 1) * GSLOTS)
+            nc.vector.tensor_copy(xsg[:, cols], xs[:].indirect(offs_sb[:, g * 32 : (g + 1) * 32]))
+
+        def move_scales():
+            for r in range(4):
+                nc.sync.dma_start(xsg_moved[r:P:32, :].bitcast(I32), xsg[4 + r : P : 32, :].bitcast(I32))
 
         def load_wq(g):
             src = wq_words[g * GROUP : (g + 1) * GROUP].rearrange("e s p b -> p (e s) b")
             nc.sync.dma_start(wq_sb[g][:].bitcast(I32), src.bitcast(I32))
 
-        def load_wk(g):
-            src = wk_words[g * GROUP : (g + 1) * GROUP].rearrange("e s p n d -> p (e s) (n d)")
-            nc.sync.dma_start(wk_sb[g][:].bitcast(I32), src.bitcast(I32))
+        wk_sb = {}
 
-        def evacuate(m, e, acc, column):
-            nc.scalar.activation(y[m][:, e * C : (e + 1) * C], acc, IDENTITY, bias=column)
+        def load_wk(first, count, halves, slot):
+            width = len(halves) * P
+            tile = keep.tile([P, count * PASSES, width], U32, name=slot, align_bytes=64)
+            src = wk_words[first : first + count].rearrange("e s p n d -> p (e s) (n d)").bitcast(I32)
+            nc.sync.dma_start(tile[:].bitcast(I32), src[:, :, halves[0] * P : halves[0] * P + width])
+            for i in range(count):
+                for h in halves:
+                    wk_sb[first + i, h] = (tile, i, (h - halves[0]) * P)
 
-        def project_packed(first_m, g, h, bank, members=range(GROUP)):
+        def evacuate(m, e, acc):
+            nc.scalar.activation(y[m][:, e * C : (e + 1) * C], acc, IDENTITY, bias=bias_sb[:, m, e : e + 1])
+
+        def project_packed(first_m, h, experts, bank):
             acc = banks[bank]
             cols = slice(h * P, (h + 1) * P)
-            for i in members:
-                e = g * GROUP + i
+            for i, e in enumerate(experts):
                 slots = slice(e * C, (e + 1) * C)
                 for s in range(PASSES):
                     if first_m == 0:
-                        lhsT = wq_sb[g][:, i * PASSES + s, 2 * h * P : 2 * (h + 1) * P].bitcast(FP4X4)
+                        row = (e % GROUP) * PASSES + s
+                        lhsT = wq_sb[e // GROUP][:, row, 2 * h * P : 2 * (h + 1) * P].bitcast(FP4X4)
                         lhsT_scale = planes[:, e * PASSES + s, cols]
+                        rhs_scale = (xsg, xsg_moved)[s][:, slots]
                     else:
-                        lhsT = wk_sb[g][:, i * PASSES + s, cols].bitcast(FP8X4)
+                        tile, place, column = wk_sb[e, h]
+                        lhsT = tile[:, place * PASSES + s, column : column + P].bitcast(FP8X4)
                         lhsT_scale = planes[4:P, e * PASSES + s, cols]
+                        rhs_scale = xsg[4 * s : P, slots]
                     nc.tensor.matmul_mx(
                         acc[:, i, :], lhsT=lhsT, lhsT_scale=lhsT_scale, rhs=xg[s][:, slots].bitcast(FP8X4),
-                        rhs_scale=xsg[s][:, slots], start=(s == 0), stop=(s == PASSES - 1),
+                        rhs_scale=rhs_scale, start=(s == 0), stop=(s == PASSES - 1),
                     )
-            for i in members:
-                e = g * GROUP + i
-                evacuate(first_m + h, e, acc[:, i, :], bias_qk[:, first_m + h, e : e + 1])
+            for i, e in enumerate(experts):
+                evacuate(first_m + h, e, acc[:, i, :])
 
         raw = {}
 
@@ -132,59 +145,21 @@ def tile_moe_qkv_kernel(
             else:
                 nc.sync.dma_start(dst, src)
 
-        def load_wv_half(e, h):
-            raw[e, h] = keep.tile([P, PASSES, 4, P], F32, name="wv%d%s" % (e, "b" * h), align_bytes=64)
-            src = wv[e].rearrange("(s p j) n -> p s j n", p=P, j=4)
-            for s in range(PASSES):
-                nc.sync.dma_start(raw[e, h][:, s, :, :], src[:, s, :, h * P : (h + 1) * P])
+        def v_accs(e):
+            if e >= E - 2:
+                return [banks[6 + h][:, e - E + 2, :] for h in range(2)]
+            return [banks[2 * (e // GROUP) + h][:, e % GROUP, :] for h in range(2)]
 
-        def project_v_half(e, h, vector_passes):
-            rounded = ring.tile([P, PASSES, P, 4], BF16, name="rounded", bufs=RBUFS, align_bytes=64)
-            for s in range(PASSES):
-                run = 2 if s in vector_passes else 4
-                dst = rounded[:, s, :, :].rearrange("p (c i) j -> p c j i", i=run)
-                src = raw[e, h][:, s, :, :].rearrange("p j (c i) -> p c j i", i=run)
-                if s in vector_passes:
-                    nc.vector.tensor_copy(dst, src)
-                else:
-                    nc.scalar.copy(dst, src)
-            codes = ring.tile([P, PASSES, P], U32, name="codes", bufs=CBUFS, align_bytes=64)
-            plane = ring.tile([P, PASSES, P], U8, name="plane", bufs=CBUFS, align_bytes=64)
-            nc.vector.quantize_mx(
-                codes[:].rearrange("p s n -> p (s n)").bitcast(FP8X4),
-                plane[:].rearrange("p s n -> p (s n)"),
-                rounded[:].rearrange("p s n j -> p (s n j)"),
-            )
-            slots = slice(e * C, (e + 1) * C)
-            for s in range(PASSES):
-                nc.tensor.matmul_mx(
-                    v_accs(e)[h], lhsT=codes[:, s, :].bitcast(FP8X4), lhsT_scale=plane[:, s, :],
-                    rhs=xg[s][:, slots].bitcast(FP8X4), rhs_scale=xsg[s][:, slots],
-                    start=(s == 0), stop=(s == PASSES - 1),
-                )
-
-        rounded_of = {}
-
-        def round_v(e, pieces):
+        def project_v(e, pieces, spans):
             rounded = ring.tile([P, PASSES, N, 4], BF16, name="rounded", bufs=RBUFS, align_bytes=64)
             for s, cols, on_vector in pieces:
-                run = 2 if on_vector else 4
-                dst = rounded[:, s, cols, :].rearrange("p (c i) j -> p c j i", i=run)
-                src = raw[e][:, s, :, cols].rearrange("p j (c i) -> p c j i", i=run)
+                dst = rounded[:, s, cols, :].rearrange("p (c i) j -> p c j i", i=4)
+                src = raw[e][:, s, :, cols].rearrange("p j (c i) -> p c j i", i=4)
                 if on_vector:
                     nc.vector.tensor_copy(dst, src)
                 else:
                     nc.scalar.copy(dst, src)
-            rounded_of[e] = rounded
-
-        quantised = {}
-
-        def quantise_v(e, spans):
-            rounded = rounded_of[e]
-            if e == 0:
-                codes = keep.tile([P, PASSES, N], U32, name="xs", align_bytes=64)
-            else:
-                codes = ring.tile([P, PASSES, N], U32, name="codes", bufs=CBUFS, align_bytes=64)
+            codes = ring.tile([P, PASSES, N], U32, name="codes", bufs=CBUFS, align_bytes=64)
             plane = ring.tile([P, PASSES, N], U8, name="plane", bufs=CBUFS, align_bytes=64)
             code_row = codes[:].rearrange("p s n -> p (s n)")
             plane_row = plane[:].rearrange("p s n -> p (s n)")
@@ -193,10 +168,6 @@ def tile_moe_qkv_kernel(
                 nc.vector.quantize_mx(
                     code_row[:, first:last].bitcast(FP8X4), plane_row[:, first:last], value_row[:, 4 * first : 4 * last]
                 )
-            quantised[e] = (codes, plane)
-
-        def project_v(e):
-            codes, plane = quantised[e]
             accs = v_accs(e)
             slots = slice(e * C, (e + 1) * C)
             for h in range(2):
@@ -204,153 +175,105 @@ def tile_moe_qkv_kernel(
                 for s in range(PASSES):
                     nc.tensor.matmul_mx(
                         accs[h], lhsT=codes[:, s, cols].bitcast(FP8X4), lhsT_scale=plane[:, s, cols],
-                        rhs=xg[s][:, slots].bitcast(FP8X4), rhs_scale=xsg[s][:, slots],
+                        rhs=xg[s][:, slots].bitcast(FP8X4), rhs_scale=xsg[4 * s : P, slots],
                         start=(s == 0), stop=(s == PASSES - 1),
                     )
 
-        def v_accs(e):
-            if e == E - 1:
-                return [banks[4 + h][:, 0, :] for h in range(2)]
-            return [banks[(6 + 2 * (e // GROUP) + h) % 8][:, e % GROUP, :] for h in range(2)]
+        def evacuate_on_vector(m, first, count, bank):
+            dst = y[m][:, first * C : (first + count) * C].rearrange("p (i c) -> p i c", c=C)
+            columns = bias_sb[:, m, first : first + count].unsqueeze(2).to_broadcast([P, count, C])
+            nc.vector.tensor_tensor(dst, banks[bank][:, :count, :], columns, ADD)
 
-        def evacuate_v(experts, halves=(0, 1)):
-            for h in halves:
-                for e in experts:
-                    evacuate(4 + h, e, v_accs(e)[h], bias_v[e // GROUP][:, h, e % GROUP : e % GROUP + 1])
-
-        def combine(m, first_token, width, slot):
-            cols = slice(first_token, first_token + width)
-            lcols = slice(first_token // 16, (first_token + width) // 16)
-            pair = keep.tile([P, 2, width], F32, name=slot, align_bytes=64)
-            for r in range(2):
-                weights = gate_sb[:, r * T + first_token : r * T + first_token + width]
-                nc.vector.tensor_tensor(pair[:, r, :], y[m][:].indirect(pos_sb[r][:, lcols]), weights, MULT)
-            nc.vector.tensor_tensor(pair[:, 0, :], pair[:, 0, :], pair[:, 1, :], ADD)
-            nc.sync.dma_start(out[m * P : (m + 1) * P, cols], pair[:, 0, :])
-
-        def combine_on_tensor(m, first_token, width, slot, sum_bank, back_bank):
-            cols = slice(first_token, first_token + width)
-            lcols = slice(first_token // 16, (first_token + width) // 16)
-            chunks = width // P
-            trio = keep.tile([P, 3, width], F32, name=slot, align_bytes=64)
-            for r in range(2):
-                weights = gate_sb[:, r * T + first_token : r * T + first_token + width]
-                nc.vector.tensor_tensor(trio[:, r, :], y[m][:].indirect(pos_sb[r][:, lcols]), weights, MULT)
-            for c in range(chunks):
-                for r in range(2):
-                    nc.tensor.matmul(
-                        banks[sum_bank][:, c, :], lhsT=trio[:, r, c * P : (c + 1) * P], rhs=identity[:],
-                        is_transpose=True, start=(r == 0), stop=(r == 1),
-                    )
-            nc.scalar.copy(trio[:, 2, :], banks[sum_bank][:, :chunks, :].rearrange("p c n -> p (c n)"))
-            for c in range(chunks):
-                nc.tensor.transpose(banks[back_bank][:, c, :], trio[:, 2, c * P : (c + 1) * P], identity[:])
-            nc.scalar.copy(trio[:, 0, :], banks[back_bank][:, :chunks, :].rearrange("p c n -> p (c n)"))
-            nc.scalar.dma_start(out[m * P : (m + 1) * P, cols], trio[:, 0, :])
+        def combine(m, slot, widths):
+            pair = keep.tile([P, 2, T], F32, name=slot, align_bytes=64)
+            first = 0
+            for width in widths:
+                cols = slice(first, first + width)
+                lcols = slice(first // 16, (first + width) // 16)
+                nc.scalar.activation(pair[:, 1, cols], y[m][:].indirect(pos_sb[1][:, lcols]), COPY)
+                nc.vector.tensor_tensor(pair[:, 0, cols], y[m][:].indirect(pos_sb[0][:, lcols]), gate_sb[:, cols], MULT)
+                first += width
+            first = 0
+            for width in widths:
+                halves = [slice(first, first + width // 2), slice(first + width // 2, first + width)]
+                for cols in halves:
+                    second_gate = gate_sb[:, T + cols.start : T + cols.stop]
+                    nc.vector.tensor_tensor(pair[:, 1, cols], pair[:, 1, cols], second_gate, MULT)
+                for cols in halves:
+                    nc.vector.tensor_tensor(pair[:, 0, cols], pair[:, 0, cols], pair[:, 1, cols], ADD)
+                nc.sync.dma_start(out[m * P : (m + 1) * P, first : first + width], pair[:, 0, first : first + width])
+                first += width
 
         def load_x(s):
             nc.sync.dma_start(xw[s][:].bitcast(I32), x_words[s].rearrange("p t d -> p (t d)").bitcast(I32))
 
         def load_x_scales():
-            x_by_row = x_scales.rearrange("s (q r) t -> r q s t", r=4)
-            for r in range(4):
-                nc.sync.dma_start(xs[r:P:32, :, :].bitcast(I32), x_by_row[r].bitcast(I32))
-
-        def load_gate():
-            nc.sync.dma_start(gate_rows[0:16, :RUN], gate[:, 0, :].rearrange("r (c j) -> r c j", j=RUN))
-
-        bias_rows = bias.rearrange("(m p) e -> p m e", p=P)
-
-        def load_small():
-            nc.sync.dma_start(bias_qk[:, :, :E], bias_rows[:, :4, :])
-            for r, pos in enumerate((pos1, pos2)):
-                nc.sync.dma_start(pos_sb[r][:], pos)
-
-        def load_bias_v(g):
-            nc.sync.dma_start(bias_v[g][:, :, :GROUP], bias_rows[:, 4:, g * GROUP : (g + 1) * GROUP])
+            for q in range(4):
+                rows = x_scales[:, 4 * q : 4 * q + 4, :]
+                nc.sync.dma_start(xs[32 * q : 32 * q + 8, :].bitcast(I32), rows.bitcast(I32))
 
         whole, low, high = slice(0, N), slice(0, P), slice(P, N)
         on_scalar = [(0, whole, False), (1, whole, False)]
-        shared = [(0, whole, False), (1, whole, True)]
-        finest = [(0, whole, False), (1, low, True), (1, high, False)]
+        shared = [(0, whole, False), (1, low, False), (1, high, True)]
+        finest = [(0, low, True), (0, high, False), (1, low, True), (1, high, False)]
         at_once = [(0, 2 * N)]
         in_three = [(0, N), (N, N + P), (N + P, 2 * N)]
 
         nc.sync.dma_start(offs_sb[:], offs)
+        nc.sync.dma_start(gate_rows[0:16, :RUN], gate[:, 0, :].rearrange("r (c j) -> r c j", j=RUN))
         load_x(0)
         load_x(1)
         load_wv(0)
-        load_gate()
         load_x_scales()
-        load_planes(0, wq_scales)
-        load_planes(4, wk_scales)
-        load_wq(0)
-        load_small()
-        load_wq(1)
-        load_wq(2)
         load_wv(1)
-        load_wk(0)
-        load_wk(1)
-        load_wk(2)
-        load_wv(2)
-        load_wv(3)
-        load_wv(4)
-        load_wv(5)
-        load_bias_v(0)
-        load_wv(6)
-        load_wv(7)
-        load_wv(8)
-        load_wv(9)
-        load_bias_v(1)
-        load_wv_half(10, 0)
-        load_wv_half(11, 0)
-        load_bias_v(2)
-        load_wv_half(10, 1)
-        load_wv_half(11, 1)
+        nc.sync.dma_start(bias_sb[:, :, :E], bias.rearrange("(m p) e -> p m e", p=P))
+        for r, pos in enumerate((pos1, pos2)):
+            nc.sync.dma_start(pos_sb[r][:], pos)
+        for e in range(2, E):
+            load_wv(e, by_pass=(e == E - 1))
 
         spread_gate()
-        for s in range(PASSES):
-            gather_words(s)
-        for first, last in ((0, 4), (4, 8), (8, 10), (10, 12)):
-            gather_scales(first * C, last * C)
-        round_v(0, on_scalar)
-        for g in range(GROUPS - 1):
-            for h in range(2):
-                project_packed(0, g, h, 2 + 2 * g + h)
-        for h in range(2):
-            project_packed(0, 2, h, 6 + h, (0, 1))
-            project_packed(0, 2, h, h, (2, 3))
-        for e in range(1, 2):
-            round_v(e, on_scalar)
-        quantise_v(0, at_once)
-        combine(0, 0, T, "wv0")
-        for e in range(1, 2):
-            quantise_v(e, at_once)
-        combine(1, 0, T, "xw0")
+        for g in range(GROUPS):
+            gather_words(0, g)
+        for g in range(GROUPS):
+            gather_words(1, g)
+            gather_scales(g)
+        for e in range(E - 1):
+            project_v(e, shared if e >= SHARED_FROM else on_scalar, at_once)
+            if e in (3, 7, 9):
+                first = e // GROUP * GROUP
+                for h in range(2):
+                    evacuate_on_vector(4 + h, first, e + 1 - first, 2 * (e // GROUP) + h)
+        project_v(E - 1, finest, in_three)
+        evacuate_on_vector(4, E - 2, 2, 6)
+        for e in range(E - 2, E):
+            evacuate(5, e, v_accs(e)[1])
+
+        move_scales()
+        load_planes(0, wq_scales)
+        load_planes(4, wk_scales)
+        for g in range(GROUPS):
+            load_wq(g)
+        load_wk(0, 4, (0, 1), "wv0")
+        load_wk(4, 4, (0,), "wv1")
+        load_wk(8, 4, (0,), "wv2")
+        load_wk(4, 4, (1,), "wv3")
+        load_wk(8, 2, (1,), "wv4")
+        load_wk(10, 2, (1,), "wv5")
+
+        combine(4, "wv6", (T,))
+        combine(5, "wv7", (T,))
         for g in range(GROUPS):
             for h in range(2):
-                project_packed(2, g, h, 2 + 2 * g + h)
-        for e in range(2):
-            project_v(e)
-        for e in range(2, 10):
-            round_v(e, shared if e >= 7 else on_scalar)
-            quantise_v(e, at_once)
-            project_v(e)
-            if e < 2 + 4:
-                combine(2 + (e - 2) // 2, ((e - 2) % 2) * T // 2, T // 2, "wv%d" % (e - 1))
-            if e == 5:
-                evacuate_v(range(0, 4))
-            if e == 9:
-                evacuate_v(range(4, 8))
-        for e in range(10, E):
-            project_v_half(e, 0, (1,))
-        evacuate_v(range(8, 11), (0,))
-        evacuate_v((11,), (0,))
-        for e in range(10, E):
-            project_v_half(e, 1, (1,))
-        evacuate_v(range(8, 11), (1,))
-        evacuate_v((11,), (1,))
-        combine_on_tensor(4, 0, T // 2, "wv5", 6, 7)
-        combine_on_tensor(4, T // 2, T // 2, "wv6", 0, 1)
-        combine(5, 0, 512, "wv0")
-        combine(5, 512, 256, "wv1")
+                project_packed(0, h, range(g * GROUP, (g + 1) * GROUP), 2 * g + h)
+        combine(0, "wv8", (T,))
+        combine(1, "wv9", (T,))
+        project_packed(2, 0, range(0, 4), 6)
+        project_packed(2, 1, range(0, 4), 7)
+        project_packed(2, 0, range(4, 8), 0)
+        project_packed(2, 0, range(8, 12), 1)
+        combine(2, "wv10", (T,))
+        project_packed(2, 1, range(4, 8), 2)
+        project_packed(2, 1, range(8, 10), 3)
+        project_packed(2, 1, range(10, 12), 4)
+        combine(3, "wv11", (512, 256))

@@ -29,6 +29,7 @@ RUN = 96
 RBUFS = 7
 CBUFS = 4
 SHARED_FROM = 4
+SPLIT = 512
 
 
 def tile_moe_qkv_kernel(
@@ -49,9 +50,12 @@ def tile_moe_qkv_kernel(
         xg = [keep.tile([P, S], U32, name="xg%d" % s, align_bytes=64) for s in range(PASSES)]
         xsg = keep.tile([P, S], U8, name="xsg", align_bytes=64)
         xsg_moved = keep.tile([P, S], U8, name="xsg_moved", align_bytes=64)
-        planes = keep.tile([P, E * PASSES, N], U8, name="planes", align_bytes=64)
+        q_planes = keep.tile([P, E * PASSES, N], U8, name="q_planes", align_bytes=64)
+        k_planes = keep.tile([P, E * PASSES, N], U8, name="k_planes", align_bytes=64)
         wq_sb = [keep.tile([P, GROUP * PASSES, 2 * N], U8, name="wq%d" % g, align_bytes=64) for g in range(GROUPS)]
-        bias_sb = keep.tile([P, 6, 16], F32, name="bias_sb")
+        bias_qk = keep.tile([P, 4, 16], F32, name="bias_qk")
+        bias_v = keep.tile([P, 2, 16], F32, name="bias_v")
+        bias_of = [bias_qk[:, m, :] for m in range(4)] + [bias_v[:, h, :] for h in range(2)]
         gate_rows = keep.tile([P, P], F32, name="gate_rows")
         gate_cols = keep.tile([P, 16], F32, name="gate_cols")
         identity = keep.tile([P, P], F32, name="identity")
@@ -62,10 +66,11 @@ def tile_moe_qkv_kernel(
         nc.gpsimd.memset(xs[:].bitcast(I32), 0)
         nc.gpsimd.memset(xsg_moved[:].bitcast(I32), 0)
         nc.vector.memset(gate_rows[:], 0.0)
-        nc.vector.memset(planes[:].rearrange("p a n -> p (a n)").bitcast(I32), 0)
+        for planes in (q_planes, k_planes):
+            nc.vector.memset(planes[:].rearrange("p a n -> p (a n)").bitcast(I32), 0)
         make_identity(nc, identity[:])
 
-        def load_planes(first, scales):
+        def load_planes(planes, first, scales):
             by_row = scales.rearrange("e s (q r) n -> r q (e s) n", r=4)
             for r in range(4):
                 nc.sync.dma_start(planes[first + r : P : 32, :, :].bitcast(I32), by_row[r].bitcast(I32))
@@ -108,9 +113,9 @@ def tile_moe_qkv_kernel(
                     wk_sb[first + i, h] = (tile, i, (h - halves[0]) * P)
 
         def evacuate(m, e, acc):
-            nc.scalar.activation(y[m][:, e * C : (e + 1) * C], acc, IDENTITY, bias=bias_sb[:, m, e : e + 1])
+            nc.scalar.activation(y[m][:, e * C : (e + 1) * C], acc, IDENTITY, bias=bias_of[m][:, e : e + 1])
 
-        def project_packed(first_m, h, experts, bank):
+        def project_packed(first_m, h, experts, bank, on_vector=False):
             acc = banks[bank]
             cols = slice(h * P, (h + 1) * P)
             for i, e in enumerate(experts):
@@ -119,19 +124,22 @@ def tile_moe_qkv_kernel(
                     if first_m == 0:
                         row = (e % GROUP) * PASSES + s
                         lhsT = wq_sb[e // GROUP][:, row, 2 * h * P : 2 * (h + 1) * P].bitcast(FP4X4)
-                        lhsT_scale = planes[:, e * PASSES + s, cols]
+                        lhsT_scale = q_planes[:, e * PASSES + s, cols]
                         rhs_scale = (xsg, xsg_moved)[s][:, slots]
                     else:
                         tile, place, column = wk_sb[e, h]
                         lhsT = tile[:, place * PASSES + s, column : column + P].bitcast(FP8X4)
-                        lhsT_scale = planes[4:P, e * PASSES + s, cols]
+                        lhsT_scale = k_planes[4:P, e * PASSES + s, cols]
                         rhs_scale = xsg[4 * s : P, slots]
                     nc.tensor.matmul_mx(
                         acc[:, i, :], lhsT=lhsT, lhsT_scale=lhsT_scale, rhs=xg[s][:, slots].bitcast(FP8X4),
                         rhs_scale=rhs_scale, start=(s == 0), stop=(s == PASSES - 1),
                     )
-            for i, e in enumerate(experts):
-                evacuate(first_m + h, e, acc[:, i, :])
+            if on_vector:
+                evacuate_on_vector(first_m + h, experts[0], len(experts), bank)
+            else:
+                for i, e in enumerate(experts):
+                    evacuate(first_m + h, e, acc[:, i, :])
 
         raw = {}
 
@@ -181,28 +189,37 @@ def tile_moe_qkv_kernel(
 
         def evacuate_on_vector(m, first, count, bank):
             dst = y[m][:, first * C : (first + count) * C].rearrange("p (i c) -> p i c", c=C)
-            columns = bias_sb[:, m, first : first + count].unsqueeze(2).to_broadcast([P, count, C])
+            columns = bias_of[m][:, first : first + count].unsqueeze(2).to_broadcast([P, count, C])
             nc.vector.tensor_tensor(dst, banks[bank][:, :count, :], columns, ADD)
 
-        def combine(m, slot, widths):
+        gates = gate_sb[:].rearrange("p (r t) -> p r t", r=2)
+
+        tokens = slice(0, T)
+
+        pairs = {}
+
+        def store(m, pieces):
+            for piece in pieces:
+                nc.sync.dma_start(out[m * P : (m + 1) * P, piece], pairs[m][:, 0, piece])
+
+        def combine(m, slot, pieces):
+            fetch_and_sum(m, slot, pieces)
+            store(m, pieces)
+
+        def fetch_and_sum(m, slot, pieces):
             pair = keep.tile([P, 2, T], F32, name=slot, align_bytes=64)
-            first = 0
-            for width in widths:
-                cols = slice(first, first + width)
-                lcols = slice(first // 16, (first + width) // 16)
+            pairs[m] = pair
+            for cols in pieces:
+                lcols = slice(cols.start // 16, cols.stop // 16)
                 nc.scalar.activation(pair[:, 1, cols], y[m][:].indirect(pos_sb[1][:, lcols]), COPY)
-                nc.vector.tensor_tensor(pair[:, 0, cols], y[m][:].indirect(pos_sb[0][:, lcols]), gate_sb[:, cols], MULT)
-                first += width
-            first = 0
-            for width in widths:
-                halves = [slice(first, first + width // 2), slice(first + width // 2, first + width)]
+                nc.vector.tensor_tensor(pair[:, 0, cols], y[m][:].indirect(pos_sb[0][:, lcols]), gates[:, 0, cols], MULT)
+            for piece in pieces:
+                middle = (piece.start + piece.stop) // 2
+                halves = [slice(piece.start, middle), slice(middle, piece.stop)]
                 for cols in halves:
-                    second_gate = gate_sb[:, T + cols.start : T + cols.stop]
-                    nc.vector.tensor_tensor(pair[:, 1, cols], pair[:, 1, cols], second_gate, MULT)
+                    nc.vector.tensor_tensor(pair[:, 1, cols], pair[:, 1, cols], gates[:, 1, cols], MULT)
                 for cols in halves:
                     nc.vector.tensor_tensor(pair[:, 0, cols], pair[:, 0, cols], pair[:, 1, cols], ADD)
-                nc.sync.dma_start(out[m * P : (m + 1) * P, first : first + width], pair[:, 0, first : first + width])
-                first += width
 
         def load_x(s):
             nc.sync.dma_start(xw[s][:].bitcast(I32), x_words[s].rearrange("p t d -> p (t d)").bitcast(I32))
@@ -226,11 +243,13 @@ def tile_moe_qkv_kernel(
         load_wv(0)
         load_x_scales()
         load_wv(1)
-        nc.sync.dma_start(bias_sb[:, :, :E], bias.rearrange("(m p) e -> p m e", p=P))
-        for r, pos in enumerate((pos1, pos2)):
-            nc.sync.dma_start(pos_sb[r][:], pos)
+        bias_rows = bias.rearrange("(m p) e -> p m e", p=P)
+        nc.sync.dma_start(bias_v[:, :, :E], bias_rows[:, 4:, :])
         for e in range(2, E):
             load_wv(e, by_pass=(e == E - 1))
+        for r, pos in enumerate((pos1, pos2)):
+            nc.sync.dma_start(pos_sb[r][:], pos)
+        nc.sync.dma_start(bias_qk[:, :, :E], bias_rows[:, :4, :])
 
         spread_gate()
         for g in range(GROUPS):
@@ -250,10 +269,17 @@ def tile_moe_qkv_kernel(
             evacuate(5, e, v_accs(e)[1])
 
         move_scales()
-        load_planes(0, wq_scales)
-        load_planes(4, wk_scales)
+        load_planes(q_planes, 0, wq_scales)
         for g in range(GROUPS):
             load_wq(g)
+        groups = [range(g * GROUP, (g + 1) * GROUP) for g in range(GROUPS)]
+        whole_band = [tokens]
+        fetch_and_sum(4, "wv6", whole_band)
+        fetch_and_sum(5, "wv7", whole_band)
+        for g in range(GROUPS):
+            for h in range(2):
+                project_packed(0, h, groups[g], 2 * g + h, on_vector=(h == 1))
+        load_planes(k_planes, 4, wk_scales)
         load_wk(0, 4, (0, 1), "wv0")
         load_wk(4, 4, (0,), "wv1")
         load_wk(8, 4, (0,), "wv2")
@@ -261,19 +287,16 @@ def tile_moe_qkv_kernel(
         load_wk(8, 2, (1,), "wv4")
         load_wk(10, 2, (1,), "wv5")
 
-        combine(4, "wv6", (T,))
-        combine(5, "wv7", (T,))
-        for g in range(GROUPS):
-            for h in range(2):
-                project_packed(0, h, range(g * GROUP, (g + 1) * GROUP), 2 * g + h)
-        combine(0, "wv8", (T,))
-        combine(1, "wv9", (T,))
-        project_packed(2, 0, range(0, 4), 6)
-        project_packed(2, 1, range(0, 4), 7)
-        project_packed(2, 0, range(4, 8), 0)
-        project_packed(2, 0, range(8, 12), 1)
-        combine(2, "wv10", (T,))
-        project_packed(2, 1, range(4, 8), 2)
+        store(4, whole_band)
+        store(5, whole_band)
+        combine(0, "wv8", whole_band)
+        combine(1, "wv9", whole_band)
+        project_packed(2, 0, groups[0], 6)
+        project_packed(2, 1, groups[0], 7)
+        project_packed(2, 0, groups[1], 0)
+        project_packed(2, 0, groups[2], 1)
+        combine(2, "wv10", whole_band)
+        project_packed(2, 1, groups[1], 2)
         project_packed(2, 1, range(8, 10), 3)
         project_packed(2, 1, range(10, 12), 4)
-        combine(3, "wv11", (512, 256))
+        combine(3, "wv11", [slice(0, SPLIT), slice(SPLIT, T)])

@@ -221,6 +221,29 @@ def tile_moe_qkv_kernel(
                 for cols in halves:
                     nc.vector.tensor_tensor(pair[:, 0, cols], pair[:, 0, cols], pair[:, 1, cols], ADD)
 
+        def combine_last(m, slot):
+            pair = keep.tile([P, 2, T], F32, name=slot, align_bytes=64)
+            pairs[m] = pair
+            head, tail = slice(0, SPLIT), slice(SPLIT, T)
+
+            def gathered(r, cols):
+                return y[m][:].indirect(pos_sb[r][:, cols.start // 16 : cols.stop // 16])
+
+            nc.scalar.activation(pair[:, 1, head], gathered(1, head), COPY)
+            nc.vector.tensor_tensor(pair[:, 0, head], gathered(0, head), gates[:, 0, head], MULT)
+            for r in range(2):
+                nc.scalar.activation(pair[:, r, tail], gathered(r, tail), COPY)
+            halves = [slice(0, SPLIT // 2), slice(SPLIT // 2, SPLIT)]
+            for cols in halves:
+                nc.vector.tensor_tensor(pair[:, 1, cols], pair[:, 1, cols], gates[:, 1, cols], MULT)
+            for cols in halves:
+                nc.vector.tensor_tensor(pair[:, 0, cols], pair[:, 0, cols], pair[:, 1, cols], ADD)
+            store(m, [head])
+            for r in range(2):
+                nc.vector.tensor_tensor(pair[:, r, tail], pair[:, r, tail], gates[:, r, tail], MULT)
+            nc.vector.tensor_tensor(pair[:, 0, tail], pair[:, 0, tail], pair[:, 1, tail], ADD)
+            store(m, [tail])
+
         def load_x(s):
             nc.sync.dma_start(xw[s][:].bitcast(I32), x_words[s].rearrange("p t d -> p (t d)").bitcast(I32))
 
@@ -278,7 +301,7 @@ def tile_moe_qkv_kernel(
         fetch_and_sum(5, "wv7", whole_band)
         for g in range(GROUPS):
             for h in range(2):
-                project_packed(0, h, groups[g], 2 * g + h, on_vector=(h == 1))
+                project_packed(0, h, groups[g], 2 * g + h, on_vector=(g == 0 and h == 1))
         load_planes(k_planes, 4, wk_scales)
         load_wk(0, 4, (0, 1), "wv0")
         load_wk(4, 4, (0,), "wv1")
@@ -299,4 +322,4 @@ def tile_moe_qkv_kernel(
         project_packed(2, 1, groups[1], 2)
         project_packed(2, 1, range(8, 10), 3)
         project_packed(2, 1, range(10, 12), 4)
-        combine(3, "wv11", [slice(0, SPLIT), slice(SPLIT, T)])
+        combine_last(3, "wv11")

@@ -29,7 +29,7 @@ RUN = 96
 RBUFS = 7
 CBUFS = 4
 SHARED_FROM = 4
-SPLIT = 512
+SPLIT = 576
 
 
 def tile_moe_qkv_kernel(
@@ -259,9 +259,10 @@ def tile_moe_qkv_kernel(
         at_once = [(0, 2 * N)]
         in_three = [(0, N), (N, N + P), (N + P, 2 * N)]
 
-        nc.sync.dma_start(offs_sb[:], offs)
-        nc.sync.dma_start(gate_rows[0:16, :RUN], gate[:, 0, :].rearrange("r (c j) -> r c j", j=RUN))
         load_x(0)
+        nc.sync.dma_start(offs_sb[:], offs)
+        for r in range(2):
+            nc.sync.dma_start(gate_rows[8 * r : 8 * r + 8, :RUN], gate[r, 0, :].rearrange("(c j) -> c j", j=RUN))
         load_x(1)
         load_wv(0)
         load_x_scales()
@@ -307,8 +308,8 @@ def tile_moe_qkv_kernel(
         load_wk(4, 4, (0,), "wv1")
         load_wk(8, 4, (0,), "wv2")
         load_wk(4, 4, (1,), "wv3")
-        load_wk(8, 2, (1,), "wv4")
-        load_wk(10, 2, (1,), "wv5")
+        load_wk(8, 3, (1,), "wv4")
+        load_wk(11, 1, (1,), "wv5")
 
         store(4, whole_band)
         store(5, whole_band)
@@ -319,7 +320,7 @@ def tile_moe_qkv_kernel(
         project_packed(2, 0, groups[1], 0)
         project_packed(2, 0, groups[2], 1)
         combine(2, "wv10", whole_band)
-        project_packed(2, 1, groups[1], 2)
-        project_packed(2, 1, range(8, 10), 3)
-        project_packed(2, 1, range(10, 12), 4)
+        project_packed(2, 1, groups[1], 2, on_vector=True)
+        project_packed(2, 1, range(8, 11), 3)
+        project_packed(2, 1, range(11, 12), 4)
         combine_last(3, "wv11")

from contextlib import ExitStack

import concourse.mybir as mybir
from concourse.masks import make_identity

K, T, E, C, N = 1024, 768, 12, 128, 256
S = E * C
FLOPS = 2 * K * 3 * N * S

F32 = mybir.dt.float32
BF16 = mybir.dt.bfloat16
I32 = mybir.dt.int32
U32 = mybir.dt.uint32
U16 = mybir.dt.uint16
U8 = mybir.dt.uint8
FP8X4 = mybir.dt.float8_e4m3fn_x4
FP4X4 = mybir.dt.float4_e2m1fn_x4
MULT = mybir.AluOpType.mult
ADD = mybir.AluOpType.add
IDENTITY = mybir.ActivationFunctionType.Identity
COPY = mybir.ActivationFunctionType.Copy

P = 128
PASSES = 2
GROUP = 4
GROUPS = E // GROUP
GSLOTS = GROUP * C
RUN = 96
RBUFS = 7
CBUFS = 4
SHARED_FROM = 4
SPLIT = 576


def tile_moe_qkv_kernel(
    tc, x_words, x_scales, wq_words, wq_scales, wk_words, wk_scales, wv, bias, gate, offs, pos1, pos2, out
):
    nc = tc.nc
    with ExitStack() as ctx:
        lists = ctx.enter_context(tc.tile_pool(name="lists", bufs=1))
        keep = ctx.enter_context(tc.tile_pool(name="keep", bufs=1))
        ring = ctx.enter_context(tc.tile_pool(name="ring", bufs=1))
        psum = ctx.enter_context(tc.psum_pool(name="psum", bufs=1))

        offs_sb = lists.tile([P, S // 16], U16, name="offs_sb")
        pos_sb = [lists.tile([P, T // 16], U16, name="pos%d_sb" % r) for r in range(2)]

        xw = [keep.tile([P, T], U32, name="xw%d" % s, align_bytes=64) for s in range(PASSES)]
        xs = keep.tile([P, T], U8, name="xs", align_bytes=64)
        xg = [keep.tile([P, S], U32, name="xg%d" % s, align_bytes=64) for s in range(PASSES)]
        xsg = keep.tile([P, S], U8, name="xsg", align_bytes=64)
        xsg_moved = keep.tile([P, S], U8, name="xsg_moved", align_bytes=64)
        q_planes = keep.tile([P, E * PASSES, N], U8, name="q_planes", align_bytes=64)
        k_planes = keep.tile([P, E * PASSES, N], U8, name="k_planes", align_bytes=64)
        wq_sb = [keep.tile([P, GROUP * PASSES, 2 * N], U8, name="wq%d" % g, align_bytes=64) for g in range(GROUPS)]
        bias_qk = keep.tile([P, 4, 16], F32, name="bias_qk")
        bias_v = keep.tile([P, 2, 16], F32, name="bias_v")
        bias_of = [bias_qk[:, m, :] for m in range(4)] + [bias_v[:, h, :] for h in range(2)]
        gate_rows = keep.tile([P, P], F32, name="gate_rows")
        gate_cols = keep.tile([P, 16], F32, name="gate_cols")
        identity = keep.tile([P, P], F32, name="identity")
        gate_sb = keep.tile([P, 2 * T], F32, name="gate_sb")
        y = [keep.tile([P, S], F32, name="y%d" % m) for m in range(6)]
        banks = [psum.tile([P, GROUP, C], F32, name="bank%d" % b) for b in range(8)]

        nc.gpsimd.memset(xs[:].bitcast(I32), 0)
        nc.gpsimd.memset(xsg_moved[:].bitcast(I32), 0)
        nc.vector.memset(gate_rows[:], 0.0)
        for planes in (q_planes, k_planes):
            nc.vector.memset(planes[:].rearrange("p a n -> p (a n)").bitcast(I32), 0)
        make_identity(nc, identity[:])

        def load_planes(planes, first, scales):
            by_row = scales.rearrange("e s (q r) n -> r q (e s) n", r=4)
            for r in range(4):
                nc.sync.dma_start(planes[first + r : P : 32, :, :].bitcast(I32), by_row[r].bitcast(I32))

        def spread_gate():
            nc.tensor.transpose(banks[7][:, 0, :], gate_rows[:], identity[:])
            nc.scalar.copy(gate_cols[:], banks[7][:, 0, :16])
            for b in range(4):
                for i in range(GROUP):
                    column = gate_cols[:, GROUP * b + i : GROUP * b + i + 1]
                    nc.tensor.transpose(banks[3 + b][:, i, :], column.to_broadcast([P, P]), identity[:])
                runs = gate_sb[:, b * GROUP * RUN : (b + 1) * GROUP * RUN].rearrange("p (i j) -> p i j", j=RUN)
                nc.scalar.copy(runs, banks[3 + b][:, :, :RUN])

        def gather_words(s, g):
            cols = slice(g * GSLOTS, (g + 1) * GSLOTS)
            nc.vector.tensor_copy(xg[s][:, cols], xw[s][:].indirect(offs_sb[:, g * 32 : (g + 1) * 32]))

        def gather_scales(g):
            cols = slice(g * GSLOTS, (g + 1) * GSLOTS)
            nc.vector.tensor_copy(xsg[:, cols], xs[:].indirect(offs_sb[:, g * 32 : (g + 1) * 32]))

        def move_scales():
            for r in range(4):
                nc.sync.dma_start(xsg_moved[r:P:32, :].bitcast(I32), xsg[4 + r : P : 32, :].bitcast(I32))

        def load_wq(g):
            src = wq_words[g * GROUP : (g + 1) * GROUP].rearrange("e s p b -> p (e s) b")
            nc.sync.dma_start(wq_sb[g][:].bitcast(I32), src.bitcast(I32))

        wk_sb = {}

        def load_wk(first, count, halves, slot):
            width = len(halves) * P
            tile = keep.tile([P, count * PASSES, width], U32, name=slot, align_bytes=64)
            src = wk_words[first : first + count].rearrange("e s p n d -> p (e s) (n d)").bitcast(I32)
            nc.sync.dma_start(tile[:].bitcast(I32), src[:, :, halves[0] * P : halves[0] * P + width])
            for i in range(count):
                for h in halves:
                    wk_sb[first + i, h] = (tile, i, (h - halves[0]) * P)

        def evacuate(m, e, acc):
            nc.scalar.activation(y[m][:, e * C : (e + 1) * C], acc, IDENTITY, bias=bias_of[m][:, e : e + 1])

        def project_packed(first_m, h, experts, bank, on_vector=False):
            acc = banks[bank]
            cols = slice(h * P, (h + 1) * P)
            for i, e in enumerate(experts):
                slots = slice(e * C, (e + 1) * C)
                for s in range(PASSES):
                    if first_m == 0:
                        row = (e % GROUP) * PASSES + s
                        lhsT = wq_sb[e // GROUP][:, row, 2 * h * P : 2 * (h + 1) * P].bitcast(FP4X4)
                        lhsT_scale = q_planes[:, e * PASSES + s, cols]
                        rhs_scale = (xsg, xsg_moved)[s][:, slots]
                    else:
                        tile, place, column = wk_sb[e, h]
                        lhsT = tile[:, place * PASSES + s, column : column + P].bitcast(FP8X4)
                        lhsT_scale = k_planes[4:P, e * PASSES + s, cols]
                        rhs_scale = xsg[4 * s : P, slots]
                    nc.tensor.matmul_mx(
                        acc[:, i, :], lhsT=lhsT, lhsT_scale=lhsT_scale, rhs=xg[s][:, slots].bitcast(FP8X4),
                        rhs_scale=rhs_scale, start=(s == 0), stop=(s == PASSES - 1),
                    )
            if on_vector:
                evacuate_on_vector(first_m + h, experts[0], len(experts), bank)
            else:
                for i, e in enumerate(experts):
                    evacuate(first_m + h, e, acc[:, i, :])

        raw = {}

        def load_wv(e, by_pass=False):
            raw[e] = keep.tile([P, PASSES, 4, N], F32, name="wv%d" % e, align_bytes=64)
            src = wv[e].rearrange("(s p j) n -> p s (j n)", p=P, j=4)
            dst = raw[e][:].rearrange("p s j n -> p s (j n)")
            if by_pass:
                for s in range(PASSES):
                    nc.sync.dma_start(dst[:, s, :], src[:, s, :])
            else:
                nc.sync.dma_start(dst, src)

        def v_accs(e):
            if e >= E - 2:
                return [banks[6 + h][:, e - E + 2, :] for h in range(2)]
            return [banks[2 * (e // GROUP) + h][:, e % GROUP, :] for h in range(2)]

        def project_v(e, pieces, spans):
            rounded = ring.tile([P, PASSES, N, 4], BF16, name="rounded", bufs=RBUFS, align_bytes=64)
            for s, cols, on_vector in pieces:
                dst = rounded[:, s, cols, :].rearrange("p (c i) j -> p c j i", i=4)
                src = raw[e][:, s, :, cols].rearrange("p j (c i) -> p c j i", i=4)
                if on_vector:
                    nc.vector.tensor_copy(dst, src)
                else:
                    nc.scalar.copy(dst, src)
            codes = ring.tile([P, PASSES, N], U32, name="codes", bufs=CBUFS, align_bytes=64)
            plane = ring.tile([P, PASSES, N], U8, name="plane", bufs=CBUFS, align_bytes=64)
            code_row = codes[:].rearrange("p s n -> p (s n)")
            plane_row = plane[:].rearrange("p s n -> p (s n)")
            value_row = rounded[:].rearrange("p s n j -> p (s n j)")
            for first, last in spans:
                nc.vector.quantize_mx(
                    code_row[:, first:last].bitcast(FP8X4), plane_row[:, first:last], value_row[:, 4 * first : 4 * last]
                )
            accs = v_accs(e)
            slots = slice(e * C, (e + 1) * C)
            for h in range(2):
                cols = slice(h * P, (h + 1) * P)
                for s in range(PASSES):
                    nc.tensor.matmul_mx(
                        accs[h], lhsT=codes[:, s, cols].bitcast(FP8X4), lhsT_scale=plane[:, s, cols],
                        rhs=xg[s][:, slots].bitcast(FP8X4), rhs_scale=xsg[4 * s : P, slots],
                        start=(s == 0), stop=(s == PASSES - 1),
                    )

        def evacuate_on_vector(m, first, count, bank):
            dst = y[m][:, first * C : (first + count) * C].rearrange("p (i c) -> p i c", c=C)
            columns = bias_of[m][:, first : first + count].unsqueeze(2).to_broadcast([P, count, C])
            nc.vector.tensor_tensor(dst, banks[bank][:, :count, :], columns, ADD)

        gates = gate_sb[:].rearrange("p (r t) -> p r t", r=2)

        tokens = slice(0, T)

        pairs = {}

        def store(m, pieces):
            for piece in pieces:
                nc.sync.dma_start(out[m * P : (m + 1) * P, piece], pairs[m][:, 0, piece])

        def combine(m, slot, pieces):
            fetch_and_sum(m, slot, pieces)
            store(m, pieces)

        def fetch_and_sum(m, slot, pieces):
            pair = keep.tile([P, 2, T], F32, name=slot, align_bytes=64)
            pairs[m] = pair
            for cols in pieces:
                lcols = slice(cols.start // 16, cols.stop // 16)
                nc.scalar.activation(pair[:, 1, cols], y[m][:].indirect(pos_sb[1][:, lcols]), COPY)
                nc.vector.tensor_tensor(pair[:, 0, cols], y[m][:].indirect(pos_sb[0][:, lcols]), gates[:, 0, cols], MULT)
            for piece in pieces:
                middle = (piece.start + piece.stop) // 2
                halves = [slice(piece.start, middle), slice(middle, piece.stop)]
                for cols in halves:
                    nc.vector.tensor_tensor(pair[:, 1, cols], pair[:, 1, cols], gates[:, 1, cols], MULT)
                for cols in halves:
                    nc.vector.tensor_tensor(pair[:, 0, cols], pair[:, 0, cols], pair[:, 1, cols], ADD)

        def combine_last(m, slot):
            pair = keep.tile([P, 2, T], F32, name=slot, align_bytes=64)
            pairs[m] = pair
            head, tail = slice(0, SPLIT), slice(SPLIT, T)

            def gathered(r, cols):
                return y[m][:].indirect(pos_sb[r][:, cols.start // 16 : cols.stop // 16])

            nc.scalar.activation(pair[:, 1, head], gathered(1, head), COPY)
            nc.vector.tensor_tensor(pair[:, 0, head], gathered(0, head), gates[:, 0, head], MULT)
            for r in range(2):
                nc.scalar.activation(pair[:, r, tail], gathered(r, tail), COPY)
            halves = [slice(0, SPLIT // 2), slice(SPLIT // 2, SPLIT)]
            for cols in halves:
                nc.vector.tensor_tensor(pair[:, 1, cols], pair[:, 1, cols], gates[:, 1, cols], MULT)
            for cols in halves:
                nc.vector.tensor_tensor(pair[:, 0, cols], pair[:, 0, cols], pair[:, 1, cols], ADD)
            store(m, [head])
            for r in range(2):
                nc.vector.tensor_tensor(pair[:, r, tail], pair[:, r, tail], gates[:, r, tail], MULT)
            nc.vector.tensor_tensor(pair[:, 0, tail], pair[:, 0, tail], pair[:, 1, tail], ADD)
            store(m, [tail])

        def load_x(s):
            nc.sync.dma_start(xw[s][:].bitcast(I32), x_words[s].rearrange("p t d -> p (t d)").bitcast(I32))

        def load_x_scales():
            for q in range(4):
                rows = x_scales[:, 4 * q : 4 * q + 4, :]
                nc.sync.dma_start(xs[32 * q : 32 * q + 8, :].bitcast(I32), rows.bitcast(I32))

        whole, low, high = slice(0, N), slice(0, P), slice(P, N)
        on_scalar = [(0, whole, False), (1, whole, False)]
        shared = [(0, whole, False), (1, low, False), (1, high, True)]
        finest = [(0, low, True), (0, high, False), (1, low, True), (1, high, False)]
        at_once = [(0, 2 * N)]
        in_three = [(0, N), (N, N + P), (N + P, 2 * N)]

        load_x(0)
        nc.sync.dma_start(offs_sb[:], offs)
        for r in range(2):
            nc.sync.dma_start(gate_rows[8 * r : 8 * r + 8, :RUN], gate[r, 0, :].rearrange("(c j) -> c j", j=RUN))
        load_x(1)
        load_wv(0)
        load_x_scales()
        load_wv(1)
        bias_rows = bias.rearrange("(m p) e -> p m e", p=P)
        nc.sync.dma_start(bias_v[:, :, :E], bias_rows[:, 4:, :])
        for e in range(2, E):
            load_wv(e, by_pass=(e == E - 1))
        for r, pos in enumerate((pos1, pos2)):
            nc.sync.dma_start(pos_sb[r][:], pos)
        nc.sync.dma_start(bias_qk[:, :, :E], bias_rows[:, :4, :])

        spread_gate()
        for g in range(GROUPS):
            gather_words(0, g)
        for g in range(GROUPS):
            gather_words(1, g)
            gather_scales(g)
        for e in range(E - 1):
            project_v(e, shared if e >= SHARED_FROM else on_scalar, at_once)
            if e in (3, 7, 9):
                first = e // GROUP * GROUP
                for h in range(2):
                    evacuate_on_vector(4 + h, first, e + 1 - first, 2 * (e // GROUP) + h)
        project_v(E - 1, finest, in_three)
        evacuate_on_vector(4, E - 2, 2, 6)
        for e in range(E - 2, E):
            evacuate(5, e, v_accs(e)[1])

        move_scales()
        load_planes(q_planes, 0, wq_scales)
        for g in range(GROUPS):
            load_wq(g)
        groups = [range(g * GROUP, (g + 1) * GROUP) for g in range(GROUPS)]
        whole_band = [tokens]
        fetch_and_sum(4, "wv6", whole_band)
        fetch_and_sum(5, "wv7", whole_band)
        for g in range(GROUPS):
            for h in range(2):
                project_packed(0, h, groups[g], 2 * g + h, on_vector=(g == 0 and h == 1))
        load_planes(k_planes, 4, wk_scales)
        load_wk(0, 4, (0, 1), "wv0")
        load_wk(4, 4, (0,), "wv1")
        load_wk(8, 4, (0,), "wv2")
        load_wk(4, 4, (1,), "wv3")
        load_wk(8, 3, (1,), "wv4")
        load_wk(11, 1, (1,), "wv5")

        store(4, whole_band)
        store(5, whole_band)
        combine(0, "wv8", whole_band)
        combine(1, "wv9", whole_band)
        project_packed(2, 0, groups[0], 6)
        project_packed(2, 1, groups[0], 7)
        project_packed(2, 0, groups[1], 0)
        project_packed(2, 0, groups[2], 1)
        combine(2, "wv10", whole_band)
        project_packed(2, 1, groups[1], 2, on_vector=True)
        project_packed(2, 1, range(8, 11), 3)
        project_packed(2, 1, range(11, 12), 4)
        combine_last(3, "wv11")
